import numpy as np
import ml_dtypes


def mxq(x, axis, fmt="e4m3"):
    dtype, down = {"e4m3": (ml_dtypes.float8_e4m3fn, 7), "e5m2": (ml_dtypes.float8_e5m2, 14)}[fmt]
    v = np.moveaxis(np.asarray(x, np.float32).astype(ml_dtypes.bfloat16).astype(np.float64), axis, -1)
    blocks = v.reshape(v.shape[:-1] + (-1, 32))
    amax = np.abs(blocks).max(-1, keepdims=True)
    byte = np.maximum(np.where(amax > 0, np.frexp(amax)[1] - 1 + 127, 0) - down, 1)
    scale = np.exp2(byte - 127.0)
    codes = (blocks / scale).astype(np.float32).astype(dtype).astype(np.float64)
    return np.moveaxis((codes * scale).reshape(v.shape), -1, axis)


WIDE = False


def mx_kscale(k):
    if not WIDE:
        return np.ones(k)
    levels = np.array([10, -10, 5, -5, 0])
    if k % 512:
        return np.exp2(np.random.permutation(np.resize(levels, k // 32))).repeat(32)
    a = np.empty((k // 512, 16))
    for p in range(k // 512):
        a[p, :8] = np.random.permutation(np.resize(levels, 8))
        for g in range(8):
            far = levels[np.abs(levels - a[p, g]) >= 10]
            a[p, g + 8] = far[np.random.randint(len(far))]
    return np.exp2(a.ravel()).repeat(32)


def f64(x):
    return np.asarray(x).astype(np.float64)


def striped(idx):
    return np.tile(idx.reshape(-1, 16).T, (8, 1)).astype(np.uint16)


def unstriped(offs):
    return offs[:16].T.reshape(-1).astype(np.int64)


def relu(v):
    return np.maximum(v, 0.0)


K, T, S, H, N = 512, 4096, 2048, 512, 256


def setup_inputs():
    n = np.random.standard_normal
    s = mx_kscale(K)[:, None]
    u = mx_kscale(H)
    return {
        "xT": (n((K, S)) * s).astype(np.float32),
        "w1": (n((K, H)) / np.sqrt(K) / s * u).astype(np.float32),
        "w2": (n((H, N)) / np.sqrt(H) / u[:, None]).astype(np.float32),
        "gate": np.tile(np.random.uniform(0.2, 1.0, S), (N, 1)).astype(np.float32),
        "offs": striped(np.sort(np.random.permutation(T)[:S])),
    }


def reference(xT, w1, w2, gate, offs):
    idx = unstriped(offs)
    xq = mxq(f64(xT), 0, "e4m3")
    h = relu(mxq(f64(w1), 0, "e4m3").T @ xq)
    y = mxq(f64(w2), 0, "e4m3").T @ mxq(h, 0, "e4m3")
    out = np.zeros((N, T))
    out[:, idx] = f64(gate) * y
    return out

@@ -1,0 +1,238 @@
+from contextlib import ExitStack
+
+import concourse.mybir as mybir
+
+K, T, S, H, N = 512, 4096, 2048, 512, 256
+FLOPS = 2 * S * (K * H + H * N)
+
+F32 = mybir.dt.float32
+BF16 = mybir.dt.bfloat16
+U32 = mybir.dt.uint32
+U16 = mybir.dt.uint16
+U8 = mybir.dt.uint8
+FP8X4 = mybir.dt.float8_e4m3fn_x4
+RELU = mybir.ActivationFunctionType.Relu
+MULT = mybir.AluOpType.mult
+
+P = 128
+C = 512
+NCH = S // C
+ZCUTS = [0, 1023, 2048, 3071, 4096]
+
+
+def tile_picked_place_mlp_relu_srt_l_kernel(tc, xT, w1, w2, gate, offs, out):
+    nc = tc.nc
+    x_hbm = xT.rearrange("(p j) s -> p j s", j=4)
+    w1_hbm = w1.rearrange("(p j) c -> p j c", j=4)
+    w2_hbm = w2.rearrange("(p j) c -> p j c", j=4)
+    gate_hbm = gate.rearrange("(b p) s -> p b s", p=P)
+    out_hbm = out.rearrange("(b p) t -> b p t", p=P)
+
+    with ExitStack() as ctx:
+        keep = ctx.enter_context(tc.tile_pool(name="keep", bufs=1))
+        acc1 = ctx.enter_context(tc.psum_pool(name="acc1", bufs=6))
+        acc2 = ctx.enter_context(tc.psum_pool(name="acc2", bufs=2))
+
+        offsets = keep.tile([P, S // 16], U16, name="offsets")
+        warm = keep.tile([P, 8], F32, name="warm")
+        nc.gpsimd.memset(warm[:], 0.0)
+        nc.scalar.activation(warm[:, 0:1], warm[:, 1:2], RELU)
+
+        def load(name, shape, src):
+            t = keep.tile(shape, F32, name=name, align_bytes=64)
+            nc.sync.dma_start(out=t[:], in_=src)
+            return t
+
+        x_raw = {}
+        g_raw = {}
+        w1_raw = {}
+
+        def load_x(c):
+            x_raw[c] = load(f"x_raw{c}", [P, 4, C], x_hbm[:, :, C * c : C * c + C])
+
+        def load_xh(c, h):
+            if h == 0 or (c not in x_raw):
+                x_raw[c] = x_raw.get(c) or keep.tile([P, 4, C], F32, name=f"x_raw{c}", align_bytes=64)
+            a = 256 * h
+            nc.sync.dma_start(out=x_raw[c][:, :, a : a + 256], in_=x_hbm[:, :, C * c + a : C * c + a + 256])
+
+        def load_g(c):
+            g_raw[c] = load(f"g_raw{c}", [P, 2, C], gate_hbm[:, :, C * c : C * c + C])
+
+        def load_w1(i):
+            w1_raw[i] = load(f"w1_raw{i}", [P, 4, 256], w1_hbm[:, :, 256 * i : 256 * i + 256])
+
+        load_w1(1)
+        load_w1(0)
+        load_xh(0, 0)
+        load_xh(0, 1)
+        load_xh(1, 0)
+        load_xh(1, 1)
+        w2_raw = load("w2_raw", [P, 4, N], w2_hbm)
+        load_x(2)
+        load_x(3)
+        nc.sync.dma_start(offsets[:], offs)
+        load_g(0)
+        load_g(1)
+        load_g(2)
+        load_g(3)
+
+        windows = [keep.tile([P, T], F32, name=f"window{b}", align_bytes=64) for b in range(2)]
+        w1_g = keep.tile([P, 4, P, 4], BF16, name="w1_g", align_bytes=64)
+        w1_q = keep.tile([P, H], U32, name="w1_q", align_bytes=64)
+        w1_s = keep.tile([P, H], U8, name="w1_s", align_bytes=64)
+        w2_g = keep.tile([P, N, 4], BF16, name="w2_g", align_bytes=64)
+        w2_q = keep.tile([P, N], U32, name="w2_q", align_bytes=64)
+        w2_s = keep.tile([P, N], U8, name="w2_s", align_bytes=64)
+        x_g = [keep.tile([P, C, 4], BF16, name=f"x_g{c}", align_bytes=64) for c in range(NCH)]
+        x_q = [keep.tile([P, C], U32, name=f"x_q{c}", align_bytes=64) for c in range(NCH)]
+        x_s = [keep.tile([P, C], U8, name=f"x_s{c}", align_bytes=64) for c in range(NCH)]
+        h_g = [keep.tile([P, C, 4], BF16, name=f"h_g{c}", align_bytes=64) for c in range(NCH)]
+        h_q = [keep.tile([P, C], U32, name=f"h_q{c}", align_bytes=64) for c in range(NCH)]
+        h_s = [keep.tile([P, C], U8, name=f"h_s{c}", align_bytes=64) for c in range(NCH)]
+        y = [[keep.tile([P, C], F32, name=f"y{c}_{b}", align_bytes=64) for b in range(2)] for c in range(NCH)]
+        V, A = nc.vector.tensor_copy, nc.scalar.copy
+
+        def ix(c, a, b, copy):
+            copy(
+                out=x_g[c][:, a:b, :],
+                in_=x_raw[c][:, :, a:b].rearrange("p j n -> p n j"),
+            )
+
+        def qx(c, a=0, b=C):
+            nc.vector.quantize_mx(
+                out=x_q[c][:, a:b].bitcast(FP8X4), scales=x_s[c][:, a:b], in_=x_g[c][:, a:b, :].rearrange("p n j -> p (n j)")
+            )
+
+        def qh(c, a=0, b=C):
+            nc.vector.quantize_mx(
+                out=h_q[c][:, a:b].bitcast(FP8X4), scales=h_s[c][:, a:b], in_=h_g[c][:, a:b, :].rearrange("p n j -> p (n j)")
+            )
+
+        def iw1(i, copy):
+            copy(
+                out=w1_g[:, :, 64 * i : 64 * i + 64, :],
+                in_=w1_raw[i][:].rearrange("p j (m t) -> p t m j", t=4),
+            )
+
+        def qw1():
+            nc.vector.quantize_mx(out=w1_q[:].bitcast(FP8X4), scales=w1_s[:], in_=w1_g[:].rearrange("p t m j -> p (t m j)"))
+
+        def w2p(copy=V):
+            copy(
+                out=w2_g[:], in_=w2_raw[:].rearrange("p j n -> p n j")
+            )
+            nc.vector.quantize_mx(out=w2_q[:].bitcast(FP8X4), scales=w2_s[:], in_=w2_g[:].rearrange("p n j -> p (n j)"))
+
+        def z(i):
+            engine = nc.gpsimd if i >= 4 else nc.vector
+            a, b = ZCUTS[i % 4], ZCUTS[i % 4 + 1]
+            engine.memset(windows[i // 4][:, a:b], 0.0)
+
+        def l1(c, s, e):
+            ps = acc1.tile([P, 4, P], F32, name="ps")
+            for t in range(4):
+                nc.tensor.matmul_mx(
+                    out=ps[:, t, :],
+                    lhsT=w1_q[:, P * t : P * t + P].bitcast(FP8X4),
+                    lhsT_scale=w1_s[:, P * t : P * t + P],
+                    rhs=x_q[c][:, P * s : P * s + P].bitcast(FP8X4),
+                    rhs_scale=x_s[c][:, P * s : P * s + P],
+                    start=True,
+                    stop=True,
+                )
+            dst, src = h_g[c][:, P * s : P * s + P, :], ps[:].rearrange("p t n -> p n t")
+            if e == 1:
+                nc.vector.tensor_scalar_max(dst, src, 0.0)
+            else:
+                nc.scalar.activation(dst, src, RELU)
+
+        def l2(c, b, copy):
+            py = acc2.tile([P, C], F32, name="py")
+            nc.tensor.matmul_mx(
+                out=py[:],
+                lhsT=w2_q[:, P * b : P * b + P].bitcast(FP8X4),
+                lhsT_scale=w2_s[:, P * b : P * b + P],
+                rhs=h_q[c][:].bitcast(FP8X4),
+                rhs_scale=h_s[c][:],
+                start=True,
+                stop=True,
+            )
+            copy(out=y[c][b][:], in_=py[:])
+
+        def sc(c, b, *stores):
+            nc.vector.tensor_tensor(
+                windows[b][:].indirect(offsets[:, C // 16 * c : C // 16 * (c + 1)]), y[c][b][:], g_raw[c][:, b, :], MULT
+            )
+            for lo, hi in stores:
+                nc.sync.dma_start(out=out_hbm[b, :, lo:hi], in_=windows[b][:, lo:hi])
+
+        ix(1, 0, 128, V)
+        ix(1, 128, 256, A)
+        qx(1, 0, 256)
+        ix(0, 0, 128, V)
+        ix(0, 128, 256, A)
+        qx(0, 0, 256)
+        ix(1, 256, 384, V)
+        ix(1, 384, 512, A)
+        qx(1, 256, 512)
+        ix(0, 256, 384, V)
+        ix(0, 384, 512, A)
+        qx(0, 256, 512)
+        z(0)
+        z(1)
+        z(2)
+        z(3)
+        z(4)
+        z(5)
+        z(6)
+        z(7)
+        iw1(0, V)
+        iw1(1, A)
+        qw1()
+        ix(3, 0, 256, V)
+        qx(3, 0, 256)
+        l1(0, 2, 1)
+        l1(0, 3, 0)
+        w2p()
+        l1(0, 0, 0)
+        l1(0, 1, 0)
+        l1(1, 0, 0)
+        l1(1, 1, 0)
+        qh(0)
+        l2(0, 0, A)
+        l1(1, 2, 0)
+        l1(1, 3, 0)
+        ix(2, 0, 256, V)
+        qx(2, 0, 256)
+        qh(1)
+        l2(0, 1, A)
+        ix(2, 256, 384, V)
+        ix(2, 384, 512, A)
+        qx(2, 256, 512)
+        l2(1, 0, A)
+        l1(2, 0, 0)
+        l1(2, 1, 0)
+        ix(3, 256, 512, V)
+        qx(3, 256, 512)
+        sc(0, 0)
+        sc(1, 0, (0, 1024))
+        l1(2, 2, 0)
+        l1(2, 3, 0)
+        l2(1, 1, A)
+        sc(0, 1)
+        qh(2)
+        l1(3, 0, 0)
+        l1(3, 1, 0)
+        l1(3, 2, 0)
+        l1(3, 3, 0)
+        l2(2, 0, A)
+        sc(1, 1, (0, 1024))
+        qh(3)
+        sc(2, 0)
+        l2(2, 1, V)
+        l2(3, 0, A)
+        sc(3, 0, (1024, 4096))
+        l2(3, 1, A)
+        sc(2, 1)
+        sc(3, 1, (1024, 4096))

@@ -15,9 +15,6 @@ RELU = mybir.ActivationFunctionType.Relu
 MULT = mybir.AluOpType.mult
 
 P = 128
-C = 512
-NCH = S // C
-ZCUTS = [0, 1023, 2048, 3071, 4096]
 
 
 def tile_picked_place_mlp_relu_srt_l_kernel(tc, xT, w1, w2, gate, offs, out):
@@ -25,7 +22,6 @@ def tile_picked_place_mlp_relu_srt_l_kernel(tc, xT, w1, w2, gate, offs, out):
     x_hbm = xT.rearrange("(p j) s -> p j s", j=4)
     w1_hbm = w1.rearrange("(p j) c -> p j c", j=4)
     w2_hbm = w2.rearrange("(p j) c -> p j c", j=4)
-    gate_hbm = gate.rearrange("(b p) s -> p b s", p=P)
     out_hbm = out.rearrange("(b p) t -> b p t", p=P)
 
     with ExitStack() as ctx:
@@ -34,49 +30,6 @@ def tile_picked_place_mlp_relu_srt_l_kernel(tc, xT, w1, w2, gate, offs, out):
         acc2 = ctx.enter_context(tc.psum_pool(name="acc2", bufs=2))
 
         offsets = keep.tile([P, S // 16], U16, name="offsets")
-        warm = keep.tile([P, 8], F32, name="warm")
-        nc.gpsimd.memset(warm[:], 0.0)
-        nc.scalar.activation(warm[:, 0:1], warm[:, 1:2], RELU)
-
-        def load(name, shape, src):
-            t = keep.tile(shape, F32, name=name, align_bytes=64)
-            nc.sync.dma_start(out=t[:], in_=src)
-            return t
-
-        x_raw = {}
-        g_raw = {}
-        w1_raw = {}
-
-        def load_x(c):
-            x_raw[c] = load(f"x_raw{c}", [P, 4, C], x_hbm[:, :, C * c : C * c + C])
-
-        def load_xh(c, h):
-            if h == 0 or (c not in x_raw):
-                x_raw[c] = x_raw.get(c) or keep.tile([P, 4, C], F32, name=f"x_raw{c}", align_bytes=64)
-            a = 256 * h
-            nc.sync.dma_start(out=x_raw[c][:, :, a : a + 256], in_=x_hbm[:, :, C * c + a : C * c + a + 256])
-
-        def load_g(c):
-            g_raw[c] = load(f"g_raw{c}", [P, 2, C], gate_hbm[:, :, C * c : C * c + C])
-
-        def load_w1(i):
-            w1_raw[i] = load(f"w1_raw{i}", [P, 4, 256], w1_hbm[:, :, 256 * i : 256 * i + 256])
-
-        load_w1(1)
-        load_w1(0)
-        load_xh(0, 0)
-        load_xh(0, 1)
-        load_xh(1, 0)
-        load_xh(1, 1)
-        w2_raw = load("w2_raw", [P, 4, N], w2_hbm)
-        load_x(2)
-        load_x(3)
-        nc.sync.dma_start(offsets[:], offs)
-        load_g(0)
-        load_g(1)
-        load_g(2)
-        load_g(3)
-
         windows = [keep.tile([P, T], F32, name=f"window{b}", align_bytes=64) for b in range(2)]
         w1_g = keep.tile([P, 4, P, 4], BF16, name="w1_g", align_bytes=64)
         w1_q = keep.tile([P, H], U32, name="w1_q", align_bytes=64)
@@ -84,155 +37,169 @@ def tile_picked_place_mlp_relu_srt_l_kernel(tc, xT, w1, w2, gate, offs, out):
         w2_g = keep.tile([P, N, 4], BF16, name="w2_g", align_bytes=64)
         w2_q = keep.tile([P, N], U32, name="w2_q", align_bytes=64)
         w2_s = keep.tile([P, N], U8, name="w2_s", align_bytes=64)
-        x_g = [keep.tile([P, C, 4], BF16, name=f"x_g{c}", align_bytes=64) for c in range(NCH)]
-        x_q = [keep.tile([P, C], U32, name=f"x_q{c}", align_bytes=64) for c in range(NCH)]
-        x_s = [keep.tile([P, C], U8, name=f"x_s{c}", align_bytes=64) for c in range(NCH)]
-        h_g = [keep.tile([P, C, 4], BF16, name=f"h_g{c}", align_bytes=64) for c in range(NCH)]
-        h_q = [keep.tile([P, C], U32, name=f"h_q{c}", align_bytes=64) for c in range(NCH)]
-        h_s = [keep.tile([P, C], U8, name=f"h_s{c}", align_bytes=64) for c in range(NCH)]
-        y = [[keep.tile([P, C], F32, name=f"y{c}_{b}", align_bytes=64) for b in range(2)] for c in range(NCH)]
-        V, A = nc.vector.tensor_copy, nc.scalar.copy
+        x_g = keep.tile([P, S, 4], BF16, name="x_g", align_bytes=64)
+        x_q = keep.tile([P, S], U32, name="x_q", align_bytes=64)
+        x_s = keep.tile([P, S], U8, name="x_s", align_bytes=64)
+        h_g = keep.tile([P, S, 4], BF16, name="h_g", align_bytes=64)
+        h_q = keep.tile([P, S], U32, name="h_q", align_bytes=64)
+        h_s = keep.tile([P, S], U8, name="h_s", align_bytes=64)
+        y = keep.tile([P, 2, S], F32, name="y", align_bytes=64)
+        V, A, G = nc.vector, nc.scalar, nc.gpsimd
+        raw = {"x": [], "w1": [], "w2": [], "g": []}
 
-        def ix(c, a, b, copy):
+        def copy(e, dst, src):
+            if e is A:
+                nc.scalar.copy(out=dst, in_=src)
+            else:
+                e.tensor_copy(out=dst, in_=src)
+
+        def load(kind, a, b, shape, src):
+            t = keep.tile(shape, F32, name=f"{kind}_raw{a}", align_bytes=64)
+            nc.sync.dma_start(out=t[:], in_=src)
+            raw[kind].append((a, b, t))
+
+        def part(kind, a, b):
+            lo, hi, t = [r for r in raw[kind] if r[0] <= a and b <= r[1]][0]
+            return t[:, a - lo : b - lo] if kind == "g" else t[:, :, a - lo : b - lo]
+
+        def tab():
+            warm = keep.tile([P, 8], F32, name="warm")
+            nc.gpsimd.memset(warm[:], 0.0)
+            nc.scalar.activation(warm[:, 0:1], warm[:, 1:2], RELU)
+
+        def lw1(a, b):
+            load("w1", a, b, [P, 4, b - a], w1_hbm[:, :, a:b])
+
+        def lw2():
+            load("w2", 0, N, [P, 4, N], w2_hbm)
+
+        def lx(a, b):
+            load("x", a, b, [P, 4, b - a], x_hbm[:, :, a:b])
+
+        def lg(a, b):
+            load("g", a, b, [P, b - a], gate[0:P, a:b])
+
+        def lo():
+            nc.sync.dma_start(offsets[:], offs)
+
+        def z(w, a, b, e=V):
+            e.memset(windows[w][:, a:b], 0.0)
+
+        def iw1(a, b, e):
             copy(
-                out=x_g[c][:, a:b, :],
-                in_=x_raw[c][:, :, a:b].rearrange("p j n -> p n j"),
+                e,
+                w1_g[:, :, a // 4 : b // 4, :].rearrange("p t m j -> p m t j"),
+                part("w1", a, b).rearrange("p j (m t) -> p m t j", t=4),
             )
 
-        def qx(c, a=0, b=C):
-            nc.vector.quantize_mx(
-                out=x_q[c][:, a:b].bitcast(FP8X4), scales=x_s[c][:, a:b], in_=x_g[c][:, a:b, :].rearrange("p n j -> p (n j)")
-            )
-
-        def qh(c, a=0, b=C):
-            nc.vector.quantize_mx(
-                out=h_q[c][:, a:b].bitcast(FP8X4), scales=h_s[c][:, a:b], in_=h_g[c][:, a:b, :].rearrange("p n j -> p (n j)")
-            )
-
-        def iw1(i, copy):
-            copy(
-                out=w1_g[:, :, 64 * i : 64 * i + 64, :],
-                in_=w1_raw[i][:].rearrange("p j (m t) -> p t m j", t=4),
-            )
+        def quant(q, s, g):
+            nc.vector.quantize_mx(out=q.bitcast(FP8X4), scales=s, in_=g)
 
         def qw1():
-            nc.vector.quantize_mx(out=w1_q[:].bitcast(FP8X4), scales=w1_s[:], in_=w1_g[:].rearrange("p t m j -> p (t m j)"))
+            quant(w1_q[:], w1_s[:], w1_g[:].rearrange("p t m j -> p (t m j)"))
 
-        def w2p(copy=V):
-            copy(
-                out=w2_g[:], in_=w2_raw[:].rearrange("p j n -> p n j")
+        def iw2(a, b, e):
+            copy(e, w2_g[:, a:b, :], part("w2", a, b).rearrange("p j n -> p n j"))
+
+        def qw2():
+            quant(w2_q[:], w2_s[:], w2_g[:].rearrange("p n j -> p (n j)"))
+
+        def ix(a, b, e):
+            copy(e, x_g[:, a:b, :], part("x", a, b).rearrange("p j n -> p n j"))
+
+        def qx(a, b):
+            quant(x_q[:, a:b], x_s[:, a:b], x_g[:, a:b, :].rearrange("p n j -> p (n j)"))
+
+        def qh(a, b):
+            quant(h_q[:, a:b], h_s[:, a:b], h_g[:, a:b, :].rearrange("p n j -> p (n j)"))
+
+        def mm(dst, wq, ws, m, q, s, a, b):
+            nc.tensor.matmul_mx(
+                out=dst,
+                lhsT=wq[:, P * m : P * m + P].bitcast(FP8X4),
+                lhsT_scale=ws[:, P * m : P * m + P],
+                rhs=q[:, a:b].bitcast(FP8X4),
+                rhs_scale=s[:, a:b],
+                start=True,
+                stop=True,
             )
-            nc.vector.quantize_mx(out=w2_q[:].bitcast(FP8X4), scales=w2_s[:], in_=w2_g[:].rearrange("p n j -> p (n j)"))
 
-        def z(i):
-            engine = nc.gpsimd if i >= 4 else nc.vector
-            a, b = ZCUTS[i % 4], ZCUTS[i % 4 + 1]
-            engine.memset(windows[i // 4][:, a:b], 0.0)
-
-        def l1(c, s, e):
+        def l1(a, e=A):
             ps = acc1.tile([P, 4, P], F32, name="ps")
             for t in range(4):
-                nc.tensor.matmul_mx(
-                    out=ps[:, t, :],
-                    lhsT=w1_q[:, P * t : P * t + P].bitcast(FP8X4),
-                    lhsT_scale=w1_s[:, P * t : P * t + P],
-                    rhs=x_q[c][:, P * s : P * s + P].bitcast(FP8X4),
-                    rhs_scale=x_s[c][:, P * s : P * s + P],
-                    start=True,
-                    stop=True,
-                )
-            dst, src = h_g[c][:, P * s : P * s + P, :], ps[:].rearrange("p t n -> p n t")
-            if e == 1:
+                mm(ps[:, t, :], w1_q, w1_s, t, x_q, x_s, a, a + P)
+            dst, src = h_g[:, a : a + P, :], ps[:].rearrange("p t n -> p n t")
+            if e is V:
                 nc.vector.tensor_scalar_max(dst, src, 0.0)
             else:
                 nc.scalar.activation(dst, src, RELU)
 
-        def l2(c, b, copy):
-            py = acc2.tile([P, C], F32, name="py")
-            nc.tensor.matmul_mx(
-                out=py[:],
-                lhsT=w2_q[:, P * b : P * b + P].bitcast(FP8X4),
-                lhsT_scale=w2_s[:, P * b : P * b + P],
-                rhs=h_q[c][:].bitcast(FP8X4),
-                rhs_scale=h_s[c][:],
-                start=True,
-                stop=True,
-            )
-            copy(out=y[c][b][:], in_=py[:])
+        def l2(a, b, e=A):
+            py = acc2.tile([P, 512], F32, name="py")
+            mm(py[:], w2_q, w2_s, b, h_q, h_s, a, a + 512)
+            copy(e, y[:, b, a : a + 512], py[:])
 
-        def sc(c, b, *stores):
+        def l2h(a, e=A):
+            py = acc2.tile([P, 2, 256], F32, name="py")
+            for b in range(2):
+                mm(py[:, b, :], w2_q, w2_s, b, h_q, h_s, a, a + 256)
+            copy(e, y[:, :, a : a + 256], py[:])
+
+        def sc(a, b, blk):
             nc.vector.tensor_tensor(
-                windows[b][:].indirect(offsets[:, C // 16 * c : C // 16 * (c + 1)]), y[c][b][:], g_raw[c][:, b, :], MULT
+                windows[blk][:].indirect(offsets[:, a // 16 : b // 16]), y[:, blk, a:b], part("g", a, b), MULT
             )
-            for lo, hi in stores:
-                nc.sync.dma_start(out=out_hbm[b, :, lo:hi], in_=windows[b][:, lo:hi])
 
-        ix(1, 0, 128, V)
-        ix(1, 128, 256, A)
-        qx(1, 0, 256)
-        ix(0, 0, 128, V)
-        ix(0, 128, 256, A)
-        qx(0, 0, 256)
-        ix(1, 256, 384, V)
-        ix(1, 384, 512, A)
-        qx(1, 256, 512)
-        ix(0, 256, 384, V)
-        ix(0, 384, 512, A)
-        qx(0, 256, 512)
-        z(0)
-        z(1)
-        z(2)
-        z(3)
-        z(4)
-        z(5)
-        z(6)
-        z(7)
-        iw1(0, V)
-        iw1(1, A)
+        def st(blk, a, b):
+            nc.sync.dma_start(out=out_hbm[blk, :, a:b], in_=windows[blk][:, a:b])
+
+        tab()
+        lw1(0, 512)
+        lx(0, 256)
+        lx(256, 512)
+        lx(512, 768)
+        lx(768, 1024)
+        lw2()
+        lx(1024, 1536)
+        lx(1536, 2048)
+        lo()
+        lg(0, 1024)
+        lg(1024, 2048)
+        iw1(0, 256, V)
+        iw1(256, 384, V)
+        iw1(384, 512, A)
         qw1()
-        ix(3, 0, 256, V)
-        qx(3, 0, 256)
-        l1(0, 2, 1)
-        l1(0, 3, 0)
-        w2p()
-        l1(0, 0, 0)
-        l1(0, 1, 0)
-        l1(1, 0, 0)
-        l1(1, 1, 0)
-        qh(0)
-        l2(0, 0, A)
-        l1(1, 2, 0)
-        l1(1, 3, 0)
-        ix(2, 0, 256, V)
-        qx(2, 0, 256)
-        qh(1)
-        l2(0, 1, A)
-        ix(2, 256, 384, V)
-        ix(2, 384, 512, A)
-        qx(2, 256, 512)
-        l2(1, 0, A)
-        l1(2, 0, 0)
-        l1(2, 1, 0)
-        ix(3, 256, 512, V)
-        qx(3, 256, 512)
-        sc(0, 0)
-        sc(1, 0, (0, 1024))
-        l1(2, 2, 0)
-        l1(2, 3, 0)
-        l2(1, 1, A)
-        sc(0, 1)
-        qh(2)
-        l1(3, 0, 0)
-        l1(3, 1, 0)
-        l1(3, 2, 0)
-        l1(3, 3, 0)
-        l2(2, 0, A)
-        sc(1, 1, (0, 1024))
-        qh(3)
-        sc(2, 0)
-        l2(2, 1, V)
-        l2(3, 0, A)
-        sc(3, 0, (1024, 4096))
-        l2(3, 1, A)
-        sc(2, 1)
-        sc(3, 1, (1024, 4096))
+        eng = [(V, A), (V, A), (V, A), (V, A), (V, V), (V, A), (V, V), (V, A)]
+        def front(a):
+            ix(a, a + 128, eng[a // 256][0])
+            ix(a + 128, a + 256, eng[a // 256][1])
+            qx(a, a + 256)
+        def mid(a):
+            l1(a)
+            l1(a + 128)
+            qh(a, a + 256)
+        for a in range(0, 2048, 256):
+            front(a)
+        iw2(0, 128, V)
+        iw2(128, 256, V)
+        qw2()
+        for a in range(0, 1024, 256):
+            mid(a)
+        l2(0, 0)
+        l2(512, 0)
+        l2(0, 1)
+        for a in range(1024, 2048, 256):
+            mid(a)
+        l2(512, 1)
+        l2(1024, 0)
+        l2(1536, 0)
+        l2(1024, 1)
+        l2(1536, 1)
+        for w in (0, 1):
+            for a, b in ((0, 1023), (1023, 2048), (2048, 3071), (3071, 4096)):
+                z(w, a, b, (V, G)[w])
+        for lo_e, cols in ((0, (0, 1024)), (1024, (1024, 4096))):
+            for blk in (0, 1):
+                sc(lo_e, lo_e + 512, blk)
+                sc(lo_e + 512, lo_e + 1024, blk)
+                st(blk, *cols)

@@ -107,6 +107,12 @@ def tile_picked_place_mlp_relu_srt_l_kernel(tc, xT, w1, w2, gate, offs, out):
         def ix(a, b, e):
             copy(e, x_g[:, a:b, :], part("x", a, b).rearrange("p j n -> p n j"))
 
+        def ixs(a, w, v, e):
+            if e is V and v > 0:
+                ix(a, a + v, V)
+            if e is A and v < w:
+                ix(a + v, a + w, A)
+
         def qx(a, b):
             quant(x_q[:, a:b], x_s[:, a:b], x_g[:, a:b, :].rearrange("p n j -> p (n j)"))
 
@@ -156,23 +162,25 @@ def tile_picked_place_mlp_relu_srt_l_kernel(tc, xT, w1, w2, gate, offs, out):
         tab()
         lw1(0, 512)
         lx(0, 256)
-        lx(256, 512)
-        lx(512, 768)
-        lx(768, 1024)
+        lx(256, 768)
         lw2()
-        lx(1024, 1536)
-        lx(1536, 2048)
+        lx(768, 1280)
+        lx(1280, 1792)
+        lx(1792, 2048)
         lo()
-        lg(0, 1024)
+        lg(0, 512)
+        lg(512, 1024)
         lg(1024, 2048)
-        iw1(0, 256, V)
-        iw1(256, 384, V)
-        iw1(384, 512, A)
+        for w in (0, 1):
+            for a, b in ((0, 1023), (1023, 2048), (2048, 3071), (3071, 4096)):
+                z(w, a, b, (V, G)[w])
+        iw1(0, 352, V)
+        iw1(352, 512, A)
         qw1()
-        eng = [(V, A), (V, A), (V, A), (V, A), (V, V), (V, A), (V, V), (V, A)]
+        share = [160, 160, 160, 224, 224, 224, 224, 224]
         def front(a):
-            ix(a, a + 128, eng[a // 256][0])
-            ix(a + 128, a + 256, eng[a // 256][1])
+            ixs(a, 256, share[a // 256], V)
+            ixs(a, 256, share[a // 256], A)
             qx(a, a + 256)
         def mid(a):
             l1(a)
@@ -180,26 +188,31 @@ def tile_picked_place_mlp_relu_srt_l_kernel(tc, xT, w1, w2, gate, offs, out):
             qh(a, a + 256)
         for a in range(0, 2048, 256):
             front(a)
-        iw2(0, 128, V)
-        iw2(128, 256, V)
+        iw2(0, 256, V)
         qw2()
-        for a in range(0, 1024, 256):
-            mid(a)
+        mid(0)
+        mid(256)
+        mid(512)
+        mid(768)
         l2(0, 0)
         l2(512, 0)
+        mid(1024)
+        mid(1280)
         l2(0, 1)
-        for a in range(1024, 2048, 256):
-            mid(a)
+        mid(1536)
+        mid(1792)
         l2(512, 1)
         l2(1024, 0)
         l2(1536, 0)
         l2(1024, 1)
         l2(1536, 1)
-        for w in (0, 1):
-            for a, b in ((0, 1023), (1023, 2048), (2048, 3071), (3071, 4096)):
-                z(w, a, b, (V, G)[w])
-        for lo_e, cols in ((0, (0, 1024)), (1024, (1024, 4096))):
-            for blk in (0, 1):
-                sc(lo_e, lo_e + 512, blk)
-                sc(lo_e + 512, lo_e + 1024, blk)
-                st(blk, *cols)
+        sc(0, 512, 0)
+        sc(512, 1024, 0)
+        st(0, 0, 1024)
+        sc(0, 512, 1)
+        sc(512, 1024, 1)
+        st(1, 0, 1024)
+        sc(1024, 2048, 0)
+        st(0, 1024, 4096)
+        sc(1024, 2048, 1)
+        st(1, 1024, 4096)

@@ -53,6 +53,9 @@ def tile_picked_place_mlp_relu_srt_l_kernel(tc, xT, w1, w2, gate, offs, out):
             else:
                 e.tensor_copy(out=dst, in_=src)
 
+        def weave(e, dst, src):
+            copy(e, dst.rearrange("p (c i) j -> p c j i", i=4), src.rearrange("p j (c i) -> p c j i", i=4))
+
         def load(kind, a, b, shape, src):
             t = keep.tile(shape, F32, name=f"{kind}_raw{a}", align_bytes=64)
             nc.sync.dma_start(out=t[:], in_=src)
@@ -99,13 +102,13 @@ def tile_picked_place_mlp_relu_srt_l_kernel(tc, xT, w1, w2, gate, offs, out):
             quant(w1_q[:], w1_s[:], w1_g[:].rearrange("p t m j -> p (t m j)"))
 
         def iw2(a, b, e):
-            copy(e, w2_g[:, a:b, :], part("w2", a, b).rearrange("p j n -> p n j"))
+            weave(e, w2_g[:, a:b, :], part("w2", a, b))
 
         def qw2():
             quant(w2_q[:], w2_s[:], w2_g[:].rearrange("p n j -> p (n j)"))
 
         def ix(a, b, e):
-            copy(e, x_g[:, a:b, :], part("x", a, b).rearrange("p j n -> p n j"))
+            weave(e, x_g[:, a:b, :], part("x", a, b))
 
         def ixs(a, w, v, e):
             if e is V and v > 0:

@@ -54,7 +54,7 @@ def tile_picked_place_mlp_relu_srt_l_kernel(tc, xT, w1, w2, gate, offs, out):
                 e.tensor_copy(out=dst, in_=src)
 
         def weave(e, dst, src):
-            copy(e, dst.rearrange("p (c i) j -> p c j i", i=4), src.rearrange("p j (c i) -> p c j i", i=4))
+            copy(e, dst.rearrange("p (c i) j -> p c j i", i=2), src.rearrange("p j (c i) -> p c j i", i=2))
 
         def load(kind, a, b, shape, src):
             t = keep.tile(shape, F32, name=f"{kind}_raw{a}", align_bytes=64)

@@ -175,8 +175,8 @@ def tile_picked_place_mlp_relu_srt_l_kernel(tc, xT, w1, w2, gate, offs, out):
         lg(512, 1024)
         lg(1024, 2048)
         for w in (0, 1):
-            for a, b in ((0, 1023), (1023, 2048), (2048, 3071), (3071, 4096)):
-                z(w, a, b, (V, G)[w])
+            for a in range(0, 4096, 1024):
+                z(w, a, a + 1024)
         iw1(0, 352, V)
         iw1(352, 512, A)
         qw1()

@@ -166,8 +166,8 @@ def tile_picked_place_mlp_relu_srt_l_kernel(tc, xT, w1, w2, gate, offs, out):
         lw1(0, 512)
         lx(0, 256)
         lx(256, 768)
-        lw2()
         lx(768, 1280)
+        lw2()
         lx(1280, 1792)
         lx(1792, 2048)
         lo()
@@ -180,7 +180,7 @@ def tile_picked_place_mlp_relu_srt_l_kernel(tc, xT, w1, w2, gate, offs, out):
         iw1(0, 352, V)
         iw1(352, 512, A)
         qw1()
-        share = [160, 160, 160, 224, 224, 224, 224, 224]
+        share = [160, 160, 160, 256, 256, 256, 256, 256]
         def front(a):
             ixs(a, 256, share[a // 256], V)
             ixs(a, 256, share[a // 256], A)
@@ -189,20 +189,26 @@ def tile_picked_place_mlp_relu_srt_l_kernel(tc, xT, w1, w2, gate, offs, out):
             l1(a)
             l1(a + 128)
             qh(a, a + 256)
-        for a in range(0, 2048, 256):
-            front(a)
+        front(0)
+        front(256)
+        front(512)
+        front(768)
+        mid(0)
+        front(1024)
         iw2(0, 256, V)
         qw2()
-        mid(0)
         mid(256)
+        front(1280)
         mid(512)
+        front(1536)
         mid(768)
         l2(0, 0)
-        l2(512, 0)
+        front(1792)
         mid(1024)
+        l2(512, 0)
         mid(1280)
-        l2(0, 1)
         mid(1536)
+        l2(0, 1)
         mid(1792)
         l2(512, 1)
         l2(1024, 0)

@@ -15,13 +15,14 @@ RELU = mybir.ActivationFunctionType.Relu
 MULT = mybir.AluOpType.mult
 
 P = 128
+ZW = 64
 
 
 def tile_picked_place_mlp_relu_srt_l_kernel(tc, xT, w1, w2, gate, offs, out):
     nc = tc.nc
     x_hbm = xT.rearrange("(p j) s -> p j s", j=4)
     w1_hbm = w1.rearrange("(p j) c -> p j c", j=4)
-    w2_hbm = w2.rearrange("(p j) c -> p j c", j=4)
+    w2_hbm = w2.rearrange("(m t i) c -> i m t c", t=4, i=2)
     out_hbm = out.rearrange("(b p) t -> b p t", p=P)
 
     with ExitStack() as ctx:
@@ -44,6 +45,7 @@ def tile_picked_place_mlp_relu_srt_l_kernel(tc, xT, w1, w2, gate, offs, out):
         h_q = keep.tile([P, S], U32, name="h_q", align_bytes=64)
         h_s = keep.tile([P, S], U8, name="h_s", align_bytes=64)
         y = keep.tile([P, 2, S], F32, name="y", align_bytes=64)
+        zeros = keep.tile([P, ZW], F32, name="zeros", align_bytes=64)
         V, A, G = nc.vector, nc.scalar, nc.gpsimd
         raw = {"x": [], "w1": [], "w2": [], "g": []}
 
@@ -67,14 +69,17 @@ def tile_picked_place_mlp_relu_srt_l_kernel(tc, xT, w1, w2, gate, offs, out):
 
         def tab():
             warm = keep.tile([P, 8], F32, name="warm")
-            nc.gpsimd.memset(warm[:], 0.0)
-            nc.scalar.activation(warm[:, 0:1], warm[:, 1:2], RELU)
+            nc.gpsimd.memset(zeros[:], 0.0)
+            nc.scalar.activation(warm[:, 0:1], zeros[:, 0:1], RELU)
 
         def lw1(a, b):
             load("w1", a, b, [P, 4, b - a], w1_hbm[:, :, a:b])
 
         def lw2():
-            load("w2", 0, N, [P, 4, N], w2_hbm)
+            t = keep.tile([P, 4, N], F32, name="w2_raw", align_bytes=64)
+            for i in range(2):
+                nc.sync.dma_start(out=t[i:P:2, :, :], in_=w2_hbm[i])
+            raw["w2"].append((0, N, t))
 
         def lx(a, b):
             load("x", a, b, [P, 4, b - a], x_hbm[:, :, a:b])
@@ -88,11 +93,15 @@ def tile_picked_place_mlp_relu_srt_l_kernel(tc, xT, w1, w2, gate, offs, out):
         def z(w, a, b, e=V):
             e.memset(windows[w][:, a:b], 0.0)
 
+        def zc(w, a, b, e=V):
+            dst = windows[w][:, a:b].rearrange("p (r c) -> p r c", c=ZW)
+            copy(e, dst, zeros[:].unsqueeze(1).to_broadcast([P, (b - a) // ZW, ZW]))
+
         def iw1(a, b, e):
             copy(
                 e,
-                w1_g[:, :, a // 4 : b // 4, :].rearrange("p t m j -> p m t j"),
-                part("w1", a, b).rearrange("p j (m t) -> p m t j", t=4),
+                w1_g[:, :, a // 4 : b // 4, :].rearrange("p t (m i) j -> p m t j i", i=2),
+                part("w1", a, b).rearrange("p j (m t i) -> p m t j i", t=4, i=2),
             )
 
         def quant(q, s, g):
@@ -174,13 +183,13 @@ def tile_picked_place_mlp_relu_srt_l_kernel(tc, xT, w1, w2, gate, offs, out):
         lg(0, 512)
         lg(512, 1024)
         lg(1024, 2048)
-        for w in (0, 1):
-            for a in range(0, 4096, 1024):
-                z(w, a, a + 1024)
-        iw1(0, 352, V)
-        iw1(352, 512, A)
+        z(0, 0, 4096)
+        z(1, 0, 3072)
+        zc(1, 3072, 4096, A)
+        iw1(0, 288, V)
+        iw1(288, 512, A)
         qw1()
-        share = [160, 160, 160, 256, 256, 256, 256, 256]
+        share = [192, 96, 96, 256, 256, 192, 192, 256]
         def front(a):
             ixs(a, 256, share[a // 256], V)
             ixs(a, 256, share[a // 256], A)
@@ -192,23 +201,23 @@ def tile_picked_place_mlp_relu_srt_l_kernel(tc, xT, w1, w2, gate, offs, out):
         front(0)
         front(256)
         front(512)
-        front(768)
         mid(0)
-        front(1024)
+        front(768)
         iw2(0, 256, V)
         qw2()
         mid(256)
-        front(1280)
+        front(1024)
         mid(512)
-        front(1536)
+        front(1280)
         mid(768)
         l2(0, 0)
-        front(1792)
-        mid(1024)
         l2(512, 0)
+        front(1536)
+        mid(1024)
+        front(1792)
         mid(1280)
-        mid(1536)
         l2(0, 1)
+        mid(1536)
         mid(1792)
         l2(512, 1)
         l2(1024, 0)

@@ -22,13 +22,13 @@ def tile_picked_place_mlp_relu_srt_l_kernel(tc, xT, w1, w2, gate, offs, out):
     nc = tc.nc
     x_hbm = xT.rearrange("(p j) s -> p j s", j=4)
     w1_hbm = w1.rearrange("(p j) c -> p j c", j=4)
-    w2_hbm = w2.rearrange("(m t i) c -> i m t c", t=4, i=2)
+    w2_hbm = w2.rearrange("(p j) c -> p j c", j=4)
     out_hbm = out.rearrange("(b p) t -> b p t", p=P)
 
     with ExitStack() as ctx:
         keep = ctx.enter_context(tc.tile_pool(name="keep", bufs=1))
-        acc1 = ctx.enter_context(tc.psum_pool(name="acc1", bufs=6))
-        acc2 = ctx.enter_context(tc.psum_pool(name="acc2", bufs=2))
+        acc = ctx.enter_context(tc.psum_pool(name="acc", bufs=1))
+        banks = [acc.tile([P, 512], F32, name=f"bank{i}") for i in range(8)]
 
         offsets = keep.tile([P, S // 16], U16, name="offsets")
         windows = [keep.tile([P, T], F32, name=f"window{b}", align_bytes=64) for b in range(2)]
@@ -76,10 +76,7 @@ def tile_picked_place_mlp_relu_srt_l_kernel(tc, xT, w1, w2, gate, offs, out):
             load("w1", a, b, [P, 4, b - a], w1_hbm[:, :, a:b])
 
         def lw2():
-            t = keep.tile([P, 4, N], F32, name="w2_raw", align_bytes=64)
-            for i in range(2):
-                nc.sync.dma_start(out=t[i:P:2, :, :], in_=w2_hbm[i])
-            raw["w2"].append((0, N, t))
+            load("w2", 0, N, [P, 4, N], w2_hbm)
 
         def lx(a, b):
             load("x", a, b, [P, 4, b - a], x_hbm[:, :, a:b])
@@ -100,8 +97,8 @@ def tile_picked_place_mlp_relu_srt_l_kernel(tc, xT, w1, w2, gate, offs, out):
         def iw1(a, b, e):
             copy(
                 e,
-                w1_g[:, :, a // 4 : b // 4, :].rearrange("p t (m i) j -> p m t j i", i=2),
-                part("w1", a, b).rearrange("p j (m t i) -> p m t j i", t=4, i=2),
+                w1_g[:, :, a // 4 : b // 4, :].rearrange("p t m j -> p m t j"),
+                part("w1", a, b).rearrange("p j (m t) -> p m t j", t=4),
             )
 
         def quant(q, s, g):
@@ -142,26 +139,20 @@ def tile_picked_place_mlp_relu_srt_l_kernel(tc, xT, w1, w2, gate, offs, out):
                 stop=True,
             )
 
-        def l1(a, e=A):
-            ps = acc1.tile([P, 4, P], F32, name="ps")
+        def b1(a, bk, e=A):
+            ps = banks[bk][:].rearrange("p (t n) -> p t n", t=4)
             for t in range(4):
                 mm(ps[:, t, :], w1_q, w1_s, t, x_q, x_s, a, a + P)
-            dst, src = h_g[:, a : a + P, :], ps[:].rearrange("p t n -> p n t")
+            dst, src = h_g[:, a : a + P, :], ps.rearrange("p t n -> p n t")
             if e is V:
                 nc.vector.tensor_scalar_max(dst, src, 0.0)
             else:
                 nc.scalar.activation(dst, src, RELU)
 
-        def l2(a, b, e=A):
-            py = acc2.tile([P, 512], F32, name="py")
+        def b2(a, b, bk, e=A):
+            py = banks[bk]
             mm(py[:], w2_q, w2_s, b, h_q, h_s, a, a + 512)
             copy(e, y[:, b, a : a + 512], py[:])
-
-        def l2h(a, e=A):
-            py = acc2.tile([P, 2, 256], F32, name="py")
-            for b in range(2):
-                mm(py[:, b, :], w2_q, w2_s, b, h_q, h_s, a, a + 256)
-            copy(e, y[:, :, a : a + 256], py[:])
 
         def sc(a, b, blk):
             nc.vector.tensor_tensor(
@@ -180,50 +171,49 @@ def tile_picked_place_mlp_relu_srt_l_kernel(tc, xT, w1, w2, gate, offs, out):
         lx(1280, 1792)
         lx(1792, 2048)
         lo()
-        lg(0, 512)
-        lg(512, 1024)
+        lg(0, 1024)
         lg(1024, 2048)
         z(0, 0, 4096)
         z(1, 0, 3072)
         zc(1, 3072, 4096, A)
-        iw1(0, 288, V)
-        iw1(288, 512, A)
+        iw1(0, 352, V)
+        iw1(352, 512, A)
         qw1()
-        share = [192, 96, 96, 256, 256, 192, 192, 256]
+        share = [192, 96, 96, 256, 224, 256, 256, 192]
         def front(a):
             ixs(a, 256, share[a // 256], V)
             ixs(a, 256, share[a // 256], A)
             qx(a, a + 256)
         def mid(a):
-            l1(a)
-            l1(a + 128)
+            b1(a, (a // 128) % 8)
+            b1(a + 128, (a // 128 + 1) % 8)
             qh(a, a + 256)
         front(0)
         front(256)
         front(512)
-        mid(0)
         front(768)
         iw2(0, 256, V)
         qw2()
-        mid(256)
+        mid(0)
         front(1024)
-        mid(512)
+        mid(256)
         front(1280)
-        mid(768)
-        l2(0, 0)
-        l2(512, 0)
+        mid(512)
         front(1536)
-        mid(1024)
+        mid(768)
+        b2(0, 0, 6)
+        b2(512, 0, 7)
         front(1792)
+        mid(1024)
         mid(1280)
-        l2(0, 1)
+        b2(0, 1, 2)
         mid(1536)
         mid(1792)
-        l2(512, 1)
-        l2(1024, 0)
-        l2(1536, 0)
-        l2(1024, 1)
-        l2(1536, 1)
+        b2(512, 1, 6)
+        b2(1024, 0, 7)
+        b2(1536, 0, 0)
+        b2(1024, 1, 1)
+        b2(1536, 1, 2)
         sc(0, 512, 0)
         sc(512, 1024, 0)
         st(0, 0, 1024)

@@ -16,6 +16,25 @@ MULT = mybir.AluOpType.mult
 
 P = 128
 ZW = 64
+XL = [[0,256],[256,768],[768,1280],[1280,1792],[1792,2048]]
+W2POS = 2
+W2S = 2
+W2V = 256
+GPOS = 4
+GPOS2 = 5
+G0 = 512
+G1 = 1024
+ZA = 3072
+W1V = 352
+END = 4
+NB1 = 6
+LAG = 3
+D = 3
+HELD = []
+QH1 = 1
+YF = 1
+STEPS = [3,4,6,7,8,9]
+SHARE = [192,256,256,256,256,256,256,256]
 
 
 def tile_picked_place_mlp_relu_srt_l_kernel(tc, xT, w1, w2, gate, offs, out):
@@ -38,15 +57,14 @@ def tile_picked_place_mlp_relu_srt_l_kernel(tc, xT, w1, w2, gate, offs, out):
         w2_g = keep.tile([P, N, 4], BF16, name="w2_g", align_bytes=64)
         w2_q = keep.tile([P, N], U32, name="w2_q", align_bytes=64)
         w2_s = keep.tile([P, N], U8, name="w2_s", align_bytes=64)
-        x_g = keep.tile([P, S, 4], BF16, name="x_g", align_bytes=64)
+        stage = [keep.tile([P, 256, 4], BF16, name=f"stage{i}", align_bytes=64) for i in range(16)]
         x_q = keep.tile([P, S], U32, name="x_q", align_bytes=64)
         x_s = keep.tile([P, S], U8, name="x_s", align_bytes=64)
-        h_g = keep.tile([P, S, 4], BF16, name="h_g", align_bytes=64)
         h_q = keep.tile([P, S], U32, name="h_q", align_bytes=64)
         h_s = keep.tile([P, S], U8, name="h_s", align_bytes=64)
         y = keep.tile([P, 2, S], F32, name="y", align_bytes=64)
         zeros = keep.tile([P, ZW], F32, name="zeros", align_bytes=64)
-        V, A, G = nc.vector, nc.scalar, nc.gpsimd
+        V, A = nc.vector, nc.scalar
         raw = {"x": [], "w1": [], "w2": [], "g": []}
 
         def copy(e, dst, src):
@@ -94,6 +112,15 @@ def tile_picked_place_mlp_relu_srt_l_kernel(tc, xT, w1, w2, gate, offs, out):
             dst = windows[w][:, a:b].rearrange("p (r c) -> p r c", c=ZW)
             copy(e, dst, zeros[:].unsqueeze(1).to_broadcast([P, (b - a) // ZW, ZW]))
 
+        def zz(w, a, b, src=0):
+            nc.vector.tensor_copy(out=windows[w][:, a:b], in_=windows[src][:, 0 : b - a])
+
+        def xs(i):
+            return stage[i]
+
+        def hs(j):
+            return stage[j + D] if j + D in HELD else stage[8 + j]
+
         def iw1(a, b, e):
             copy(
                 e,
@@ -114,19 +141,14 @@ def tile_picked_place_mlp_relu_srt_l_kernel(tc, xT, w1, w2, gate, offs, out):
             quant(w2_q[:], w2_s[:], w2_g[:].rearrange("p n j -> p (n j)"))
 
         def ix(a, b, e):
-            weave(e, x_g[:, a:b, :], part("x", a, b))
-
-        def ixs(a, w, v, e):
-            if e is V and v > 0:
-                ix(a, a + v, V)
-            if e is A and v < w:
-                ix(a + v, a + w, A)
+            if b > a:
+                weave(e, xs(a // 256)[:, a % 256 : a % 256 + b - a, :], part("x", a, b))
 
         def qx(a, b):
-            quant(x_q[:, a:b], x_s[:, a:b], x_g[:, a:b, :].rearrange("p n j -> p (n j)"))
+            quant(x_q[:, a:b], x_s[:, a:b], xs(a // 256)[:].rearrange("p n j -> p (n j)"))
 
         def qh(a, b):
-            quant(h_q[:, a:b], h_s[:, a:b], h_g[:, a:b, :].rearrange("p n j -> p (n j)"))
+            quant(h_q[:, a:b], h_s[:, a:b], hs(a // 256)[:].rearrange("p n j -> p (n j)"))
 
         def mm(dst, wq, ws, m, q, s, a, b):
             nc.tensor.matmul_mx(
@@ -139,20 +161,16 @@ def tile_picked_place_mlp_relu_srt_l_kernel(tc, xT, w1, w2, gate, offs, out):
                 stop=True,
             )
 
-        def b1(a, bk, e=A):
+        def b1(a, bk):
             ps = banks[bk][:].rearrange("p (t n) -> p t n", t=4)
             for t in range(4):
                 mm(ps[:, t, :], w1_q, w1_s, t, x_q, x_s, a, a + P)
-            dst, src = h_g[:, a : a + P, :], ps.rearrange("p t n -> p n t")
-            if e is V:
-                nc.vector.tensor_scalar_max(dst, src, 0.0)
-            else:
-                nc.scalar.activation(dst, src, RELU)
+            nc.scalar.activation(hs(a // 256)[:, a % 256 : a % 256 + P, :], ps.rearrange("p t n -> p n t"), RELU)
 
-        def b2(a, b, bk, e=A):
+        def b2(a, b, bk):
             py = banks[bk]
             mm(py[:], w2_q, w2_s, b, h_q, h_s, a, a + 512)
-            copy(e, y[:, b, a : a + 512], py[:])
+            nc.scalar.copy(out=y[:, b, a : a + 512], in_=py[:])
 
         def sc(a, b, blk):
             nc.vector.tensor_tensor(
@@ -164,63 +182,73 @@ def tile_picked_place_mlp_relu_srt_l_kernel(tc, xT, w1, w2, gate, offs, out):
 
         tab()
         lw1(0, 512)
-        lx(0, 256)
-        lx(256, 768)
-        lx(768, 1280)
-        lw2()
-        lx(1280, 1792)
-        lx(1792, 2048)
-        lo()
-        lg(0, 1024)
-        lg(1024, 2048)
+        for n, (a, b) in enumerate(XL):
+            if n == W2POS:
+                lw2()
+            if n == GPOS:
+                lo()
+                lg(0, G0)
+            if n == GPOS2:
+                lg(G0, G1)
+            lx(a, b)
+        if GPOS >= len(XL):
+            lo()
+            lg(0, G0)
+        if GPOS2 >= len(XL) and G1 > G0:
+            lg(G0, G1)
+        lg(G1, 2048)
         z(0, 0, 4096)
-        z(1, 0, 3072)
-        zc(1, 3072, 4096, A)
-        iw1(0, 352, V)
-        iw1(352, 512, A)
-        qw1()
-        share = [192, 96, 96, 256, 224, 256, 256, 192]
-        def front(a):
-            ixs(a, 256, share[a // 256], V)
-            ixs(a, 256, share[a // 256], A)
-            qx(a, a + 256)
-        def mid(a):
-            b1(a, (a // 128) % 8)
-            b1(a + 128, (a // 128 + 1) % 8)
-            qh(a, a + 256)
-        front(0)
-        front(256)
-        front(512)
-        front(768)
-        iw2(0, 256, V)
-        qw2()
-        mid(0)
-        front(1024)
-        mid(256)
-        front(1280)
-        mid(512)
-        front(1536)
-        mid(768)
-        b2(0, 0, 6)
-        b2(512, 0, 7)
-        front(1792)
-        mid(1024)
-        mid(1280)
-        b2(0, 1, 2)
-        mid(1536)
-        mid(1792)
-        b2(512, 1, 6)
-        b2(1024, 0, 7)
-        b2(1536, 0, 0)
-        b2(1024, 1, 1)
-        b2(1536, 1, 2)
-        sc(0, 512, 0)
-        sc(512, 1024, 0)
-        st(0, 0, 1024)
-        sc(0, 512, 1)
-        sc(512, 1024, 1)
-        st(1, 0, 1024)
-        sc(1024, 2048, 0)
-        st(0, 1024, 4096)
-        sc(1024, 2048, 1)
-        st(1, 1024, 4096)
+        z(1, 0, ZA)
+        if ZA < 4096:
+            zc(1, ZA, 4096, A)
+        iw1(0, W1V, V)
+        if W1V < 512:
+            iw1(W1V, 512, A)
+        jobs = {1: [(0, 512, 0), (0, 512, 1), (512, 1024, 0), (512, 1024, 1), (1024, 2048, 0), (1024, 2048, 1)],
+                4: [(0, 512, 0), (512, 1024, 0), (0, 512, 1), (512, 1024, 1), (1024, 2048, 0), (1024, 2048, 1)],
+                6: [(0, 512, 0), (0, 512, 1), (512, 1024, 0), (512, 1024, 1), (1024, 1536, 0), (1536, 2048, 0), (1024, 2048, 1)],
+                7: [(0, 512, 0), (0, 512, 1), (512, 1024, 0), (1024, 1536, 0), (512, 1024, 1), (1536, 2048, 0), (1024, 2048, 1)],
+                }[END]
+        done = [0, 0]
+        nb = [0]
+
+        def l2(job):
+            for a in range(job[0], job[1], 512):
+                b2(a, job[2], NB1 + nb[0] % (8 - NB1))
+                nb[0] = nb[0] + 1
+
+        for i in range(8 + LAG + 2):
+            j = i - LAG
+            now = [job for job, s in zip(jobs, STEPS) if s == j]
+            if 0 <= j < 8 and QH1:
+                qh(256 * j, 256 * j + 256)
+            if i < 8:
+                ix(256 * i, 256 * i + SHARE[i], V)
+                ix(256 * i + SHARE[i], 256 * i + 256, A)
+            if i == 0:
+                qw1()
+            if i == W2S:
+                iw2(0, W2V, V)
+                if W2V < 256:
+                    iw2(W2V, 256, A)
+            if 0 <= j < 8 and not QH1:
+                qh(256 * j, 256 * j + 256)
+            if i < 8:
+                qx(256 * i, 256 * i + 256)
+            if i == W2S:
+                qw2()
+            if YF:
+                for job in now:
+                    l2(job)
+            if i < 8:
+                b1(256 * i, (2 * i) % NB1)
+                b1(256 * i + 128, (2 * i + 1) % NB1)
+            if not YF:
+                for job in now:
+                    l2(job)
+            for job in now:
+                sc(job[0], job[1], job[2])
+                end = 4096 if job[1] == 2048 else job[1]
+                if job[1] == 1024 or job[1] == 2048:
+                    st(job[2], done[job[2]], end)
+                    done[job[2]] = end

@@ -17,24 +17,29 @@ MULT = mybir.AluOpType.mult
 P = 128
 ZW = 64
 XL = [[0,256],[256,768],[768,1280],[1280,1792],[1792,2048]]
-W2POS = 2
-W2S = 2
-W2V = 256
-GPOS = 4
-GPOS2 = 5
+W2POS = 3
+W2S = 3
+W2V = 128
+GPOS = 5
+GPOS2 = 9
 G0 = 512
 G1 = 1024
 ZA = 3072
 W1V = 352
-END = 4
+END = 1
 NB1 = 6
-LAG = 3
+LAG = 2
 D = 3
 HELD = []
-QH1 = 1
+QH1 = 0
 YF = 1
-STEPS = [3,4,6,7,8,9]
-SHARE = [192,256,256,256,256,256,256,256]
+STEPS = [4,5,6,7,8,9]
+SHARE = [192,192,256,256,256,256,256,256]
+LA = 1
+LR = 0
+YAT = [[0,0,4,6],[512,0,6,7],[0,1,6,2],[512,1,7,4],[1024,0,8,5],[1536,0,10,0],[1024,1,10,6],[1536,1,10,2]]
+SC = [[0,512,0],[512,1024,0],[0,512,1],[512,1024,1],[1024,2048,0],[1024,2048,1]]
+XSLOT = [0,1,2,3,4,5,6,7]
 
 
 def tile_picked_place_mlp_relu_srt_l_kernel(tc, xT, w1, w2, gate, offs, out):
@@ -116,7 +121,7 @@ def tile_picked_place_mlp_relu_srt_l_kernel(tc, xT, w1, w2, gate, offs, out):
             nc.vector.tensor_copy(out=windows[w][:, a:b], in_=windows[src][:, 0 : b - a])
 
         def xs(i):
-            return stage[i]
+            return stage[XSLOT[i]]
 
         def hs(j):
             return stage[j + D] if j + D in HELD else stage[8 + j]
@@ -204,51 +209,41 @@ def tile_picked_place_mlp_relu_srt_l_kernel(tc, xT, w1, w2, gate, offs, out):
         iw1(0, W1V, V)
         if W1V < 512:
             iw1(W1V, 512, A)
-        jobs = {1: [(0, 512, 0), (0, 512, 1), (512, 1024, 0), (512, 1024, 1), (1024, 2048, 0), (1024, 2048, 1)],
-                4: [(0, 512, 0), (512, 1024, 0), (0, 512, 1), (512, 1024, 1), (1024, 2048, 0), (1024, 2048, 1)],
-                6: [(0, 512, 0), (0, 512, 1), (512, 1024, 0), (512, 1024, 1), (1024, 1536, 0), (1536, 2048, 0), (1024, 2048, 1)],
-                7: [(0, 512, 0), (0, 512, 1), (512, 1024, 0), (1024, 1536, 0), (512, 1024, 1), (1536, 2048, 0), (1024, 2048, 1)],
-                }[END]
-        done = [0, 0]
-        nb = [0]
 
-        def l2(job):
-            for a in range(job[0], job[1], 512):
-                b2(a, job[2], NB1 + nb[0] % (8 - NB1))
-                nb[0] = nb[0] + 1
+        def share_a(i):
+            if i < 8:
+                ix(256 * i + SHARE[i], 256 * i + 256, A)
 
-        for i in range(8 + LAG + 2):
+        for i in range(LA):
+            share_a(i)
+        for i in range(11):
             j = i - LAG
-            now = [job for job, s in zip(jobs, STEPS) if s == j]
-            if 0 <= j < 8 and QH1:
-                qh(256 * j, 256 * j + 256)
             if i < 8:
                 ix(256 * i, 256 * i + SHARE[i], V)
-                ix(256 * i + SHARE[i], 256 * i + 256, A)
             if i == 0:
                 qw1()
             if i == W2S:
-                iw2(0, W2V, V)
+                if W2V > 0:
+                    iw2(0, W2V, V)
                 if W2V < 256:
                     iw2(W2V, 256, A)
-            if 0 <= j < 8 and not QH1:
+            if 0 <= j < 8:
                 qh(256 * j, 256 * j + 256)
+            share_a(i + LA)
             if i < 8:
                 qx(256 * i, 256 * i + 256)
             if i == W2S:
                 qw2()
-            if YF:
-                for job in now:
-                    l2(job)
-            if i < 8:
-                b1(256 * i, (2 * i) % NB1)
-                b1(256 * i + 128, (2 * i + 1) % NB1)
-            if not YF:
-                for job in now:
-                    l2(job)
-            for job in now:
-                sc(job[0], job[1], job[2])
-                end = 4096 if job[1] == 2048 else job[1]
-                if job[1] == 1024 or job[1] == 2048:
-                    st(job[2], done[job[2]], end)
-                    done[job[2]] = end
+            r = i - LR
+            if 0 <= r < 8:
+                b1(256 * r, (2 * r) % 8)
+                b1(256 * r + 128, (2 * r + 1) % 8)
+            for n, (a, b, at, bk) in enumerate(YAT):
+                if at == i:
+                    b2(a, b, bk)
+        for a, b, blk in SC:
+            sc(a, b, blk)
+            if b == 1024:
+                st(blk, 0, 1024)
+            if b == 2048:
+                st(blk, 1024, 4096)

@@ -15,235 +15,154 @@ RELU = mybir.ActivationFunctionType.Relu
 MULT = mybir.AluOpType.mult
 
 P = 128
-ZW = 64
-XL = [[0,256],[256,768],[768,1280],[1280,1792],[1792,2048]]
-W2POS = 3
-W2S = 3
-W2V = 128
-GPOS = 5
-GPOS2 = 9
-G0 = 512
-G1 = 1024
-ZA = 3072
-W1V = 352
-END = 1
-NB1 = 6
-LAG = 2
-D = 3
-HELD = []
-QH1 = 0
-YF = 1
-STEPS = [4,5,6,7,8,9]
-SHARE = [192,192,256,256,256,256,256,256]
-LA = 1
-LR = 0
-YAT = [[0,0,4,6],[512,0,6,7],[0,1,6,2],[512,1,7,4],[1024,0,8,5],[1536,0,10,0],[1024,1,10,6],[1536,1,10,2]]
-SC = [[0,512,0],[512,1024,0],[0,512,1],[512,1024,1],[1024,2048,0],[1024,2048,1]]
-XSLOT = [0,1,2,3,4,5,6,7]
+PACK = 4
+BANKS = 8
+PIECE = 256
+CHUNK = 512
+PIECES = S // PIECE
+HALF = S // 2
+X_LOADS = ((0, 256), (256, 768), (768, 1280), (1280, 1792), (1792, 2048))
+X_LOADS_BEFORE_W2 = 3
+W2_AFTER_PIECE = 4
+SCALAR_CLEARS = 1024
+W1_VECTOR_COLUMNS = 352
+SCALAR_ENTRIES = 64
+ZERO_COLUMNS = 64
 
 
 def tile_picked_place_mlp_relu_srt_l_kernel(tc, xT, w1, w2, gate, offs, out):
     nc = tc.nc
-    x_hbm = xT.rearrange("(p j) s -> p j s", j=4)
-    w1_hbm = w1.rearrange("(p j) c -> p j c", j=4)
-    w2_hbm = w2.rearrange("(p j) c -> p j c", j=4)
-    out_hbm = out.rearrange("(b p) t -> b p t", p=P)
+    out_blocks = out.rearrange("(b p) t -> b p t", p=P)
 
     with ExitStack() as ctx:
         keep = ctx.enter_context(tc.tile_pool(name="keep", bufs=1))
         acc = ctx.enter_context(tc.psum_pool(name="acc", bufs=1))
-        banks = [acc.tile([P, 512], F32, name=f"bank{i}") for i in range(8)]
+        banks = [acc.tile([P, CHUNK], F32, name=f"bank{i}") for i in range(BANKS)]
 
         offsets = keep.tile([P, S // 16], U16, name="offsets")
         windows = [keep.tile([P, T], F32, name=f"window{b}", align_bytes=64) for b in range(2)]
-        w1_g = keep.tile([P, 4, P, 4], BF16, name="w1_g", align_bytes=64)
-        w1_q = keep.tile([P, H], U32, name="w1_q", align_bytes=64)
-        w1_s = keep.tile([P, H], U8, name="w1_s", align_bytes=64)
-        w2_g = keep.tile([P, N, 4], BF16, name="w2_g", align_bytes=64)
-        w2_q = keep.tile([P, N], U32, name="w2_q", align_bytes=64)
-        w2_s = keep.tile([P, N], U8, name="w2_s", align_bytes=64)
-        stage = [keep.tile([P, 256, 4], BF16, name=f"stage{i}", align_bytes=64) for i in range(16)]
-        x_q = keep.tile([P, S], U32, name="x_q", align_bytes=64)
-        x_s = keep.tile([P, S], U8, name="x_s", align_bytes=64)
-        h_q = keep.tile([P, S], U32, name="h_q", align_bytes=64)
-        h_s = keep.tile([P, S], U8, name="h_s", align_bytes=64)
+        w1_woven = keep.tile([P, PACK, P, PACK], BF16, name="w1_woven", align_bytes=64)
+        w1_codes = keep.tile([P, H], U32, name="w1_codes", align_bytes=64)
+        w1_scales = keep.tile([P, H], U8, name="w1_scales", align_bytes=64)
+        w2_woven = keep.tile([P, N, PACK], BF16, name="w2_woven", align_bytes=64)
+        w2_codes = keep.tile([P, N], U32, name="w2_codes", align_bytes=64)
+        w2_scales = keep.tile([P, N], U8, name="w2_scales", align_bytes=64)
+        x_woven = keep.tile([P, S, PACK], BF16, name="x_woven", align_bytes=64)
+        x_codes = keep.tile([P, S], U32, name="x_codes", align_bytes=64)
+        x_scales = keep.tile([P, S], U8, name="x_scales", align_bytes=64)
+        h_woven = keep.tile([P, S, PACK], BF16, name="h_woven", align_bytes=64)
+        h_codes = keep.tile([P, S], U32, name="h_codes", align_bytes=64)
+        h_scales = keep.tile([P, S], U8, name="h_scales", align_bytes=64)
         y = keep.tile([P, 2, S], F32, name="y", align_bytes=64)
-        zeros = keep.tile([P, ZW], F32, name="zeros", align_bytes=64)
-        V, A = nc.vector, nc.scalar
-        raw = {"x": [], "w1": [], "w2": [], "g": []}
+        zeros = keep.tile([P, ZERO_COLUMNS], F32, name="zeros", align_bytes=64)
+        warm = keep.tile([P, 8], F32, name="warm")
 
-        def copy(e, dst, src):
-            if e is A:
-                nc.scalar.copy(out=dst, in_=src)
-            else:
-                e.tensor_copy(out=dst, in_=src)
+        def load_rows(name, src):
+            raw = keep.tile([P, PACK, src.shape[1]], F32, name=name, align_bytes=64)
+            nc.sync.dma_start(out=raw[:], in_=src.rearrange("(p j) c -> p j c", j=PACK))
+            return raw
 
-        def weave(e, dst, src):
-            copy(e, dst.rearrange("p (c i) j -> p c j i", i=2), src.rearrange("p j (c i) -> p c j i", i=2))
+        def weave(copy, dst, src):
+            copy(out=dst.rearrange("p (c i) j -> p c j i", i=2), in_=src.rearrange("p j (c i) -> p c j i", i=2))
 
-        def load(kind, a, b, shape, src):
-            t = keep.tile(shape, F32, name=f"{kind}_raw{a}", align_bytes=64)
-            nc.sync.dma_start(out=t[:], in_=src)
-            raw[kind].append((a, b, t))
-
-        def part(kind, a, b):
-            lo, hi, t = [r for r in raw[kind] if r[0] <= a and b <= r[1]][0]
-            return t[:, a - lo : b - lo] if kind == "g" else t[:, :, a - lo : b - lo]
-
-        def tab():
-            warm = keep.tile([P, 8], F32, name="warm")
-            nc.gpsimd.memset(zeros[:], 0.0)
-            nc.scalar.activation(warm[:, 0:1], zeros[:, 0:1], RELU)
-
-        def lw1(a, b):
-            load("w1", a, b, [P, 4, b - a], w1_hbm[:, :, a:b])
-
-        def lw2():
-            load("w2", 0, N, [P, 4, N], w2_hbm)
-
-        def lx(a, b):
-            load("x", a, b, [P, 4, b - a], x_hbm[:, :, a:b])
-
-        def lg(a, b):
-            load("g", a, b, [P, b - a], gate[0:P, a:b])
-
-        def lo():
-            nc.sync.dma_start(offsets[:], offs)
-
-        def z(w, a, b, e=V):
-            e.memset(windows[w][:, a:b], 0.0)
-
-        def zc(w, a, b, e=V):
-            dst = windows[w][:, a:b].rearrange("p (r c) -> p r c", c=ZW)
-            copy(e, dst, zeros[:].unsqueeze(1).to_broadcast([P, (b - a) // ZW, ZW]))
-
-        def zz(w, a, b, src=0):
-            nc.vector.tensor_copy(out=windows[w][:, a:b], in_=windows[src][:, 0 : b - a])
-
-        def xs(i):
-            return stage[XSLOT[i]]
-
-        def hs(j):
-            return stage[j + D] if j + D in HELD else stage[8 + j]
-
-        def iw1(a, b, e):
+        def weave_w1(copy, a, b):
             copy(
-                e,
-                w1_g[:, :, a // 4 : b // 4, :].rearrange("p t m j -> p m t j"),
-                part("w1", a, b).rearrange("p j (m t) -> p m t j", t=4),
+                out=w1_woven[:, :, a // PACK : b // PACK, :].rearrange("p t m j -> p m t j"),
+                in_=w1_raw[:, :, a:b].rearrange("p j (m t) -> p m t j", t=PACK),
             )
 
-        def quant(q, s, g):
-            nc.vector.quantize_mx(out=q.bitcast(FP8X4), scales=s, in_=g)
+        def weave_x(copy, a, b):
+            first, raw = [(lo, t) for (lo, hi), t in zip(X_LOADS, x_raw) if lo <= a and b <= hi][0]
+            weave(copy, x_woven[:, a:b, :], raw[:, :, a - first : b - first])
 
-        def qw1():
-            quant(w1_q[:], w1_s[:], w1_g[:].rearrange("p t m j -> p (t m j)"))
+        def quantise(codes, scales, woven):
+            nc.vector.quantize_mx(out=codes.bitcast(FP8X4), scales=scales, in_=woven)
 
-        def iw2(a, b, e):
-            weave(e, w2_g[:, a:b, :], part("w2", a, b))
+        def quantise_piece(codes, scales, woven, piece):
+            cols = slice(PIECE * piece, PIECE * (piece + 1))
+            quantise(codes[:, cols], scales[:, cols], woven[:, cols, :].rearrange("p n j -> p (n j)"))
 
-        def qw2():
-            quant(w2_q[:], w2_s[:], w2_g[:].rearrange("p n j -> p (n j)"))
-
-        def ix(a, b, e):
-            if b > a:
-                weave(e, xs(a // 256)[:, a % 256 : a % 256 + b - a, :], part("x", a, b))
-
-        def qx(a, b):
-            quant(x_q[:, a:b], x_s[:, a:b], xs(a // 256)[:].rearrange("p n j -> p (n j)"))
-
-        def qh(a, b):
-            quant(h_q[:, a:b], h_s[:, a:b], hs(a // 256)[:].rearrange("p n j -> p (n j)"))
-
-        def mm(dst, wq, ws, m, q, s, a, b):
+        def product(dst, w_codes, w_scales, group, codes, scales, a, b):
             nc.tensor.matmul_mx(
                 out=dst,
-                lhsT=wq[:, P * m : P * m + P].bitcast(FP8X4),
-                lhsT_scale=ws[:, P * m : P * m + P],
-                rhs=q[:, a:b].bitcast(FP8X4),
-                rhs_scale=s[:, a:b],
+                lhsT=w_codes[:, P * group : P * (group + 1)].bitcast(FP8X4),
+                lhsT_scale=w_scales[:, P * group : P * (group + 1)],
+                rhs=codes[:, a:b].bitcast(FP8X4),
+                rhs_scale=scales[:, a:b],
                 start=True,
                 stop=True,
             )
 
-        def b1(a, bk):
-            ps = banks[bk][:].rearrange("p (t n) -> p t n", t=4)
-            for t in range(4):
-                mm(ps[:, t, :], w1_q, w1_s, t, x_q, x_s, a, a + P)
-            nc.scalar.activation(hs(a // 256)[:, a % 256 : a % 256 + P, :], ps.rearrange("p t n -> p n t"), RELU)
+        def layer1(a):
+            bank = banks[a // P % BANKS][:].rearrange("p (t n) -> p t n", t=PACK)
+            for t in range(PACK):
+                product(bank[:, t, :], w1_codes, w1_scales, t, x_codes, x_scales, a, a + P)
+            nc.scalar.activation(h_woven[:, a : a + P, :], bank.rearrange("p t n -> p n t"), RELU)
 
-        def b2(a, b, bk):
-            py = banks[bk]
-            mm(py[:], w2_q, w2_s, b, h_q, h_s, a, a + 512)
-            nc.scalar.copy(out=y[:, b, a : a + 512], in_=py[:])
+        def layer2(chunk, block, bank):
+            a = CHUNK * chunk
+            product(banks[bank][:], w2_codes, w2_scales, block, h_codes, h_scales, a, a + CHUNK)
+            nc.scalar.copy(out=y[:, block, a : a + CHUNK], in_=banks[bank][:])
 
-        def sc(a, b, blk):
+        def scatter(block, a, b):
             nc.vector.tensor_tensor(
-                windows[blk][:].indirect(offsets[:, a // 16 : b // 16]), y[:, blk, a:b], part("g", a, b), MULT
+                windows[block][:].indirect(offsets[:, a // 16 : b // 16]),
+                y[:, block, a:b],
+                gates[a // HALF][:, a % HALF : a % HALF + b - a],
+                MULT,
             )
 
-        def st(blk, a, b):
-            nc.sync.dma_start(out=out_hbm[blk, :, a:b], in_=windows[blk][:, a:b])
+        def store(block, a, b):
+            nc.sync.dma_start(out=out_blocks[block, :, a:b], in_=windows[block][:, a:b])
 
-        tab()
-        lw1(0, 512)
-        for n, (a, b) in enumerate(XL):
-            if n == W2POS:
-                lw2()
-            if n == GPOS:
-                lo()
-                lg(0, G0)
-            if n == GPOS2:
-                lg(G0, G1)
-            lx(a, b)
-        if GPOS >= len(XL):
-            lo()
-            lg(0, G0)
-        if GPOS2 >= len(XL) and G1 > G0:
-            lg(G0, G1)
-        lg(G1, 2048)
-        z(0, 0, 4096)
-        z(1, 0, ZA)
-        if ZA < 4096:
-            zc(1, ZA, 4096, A)
-        iw1(0, W1V, V)
-        if W1V < 512:
-            iw1(W1V, 512, A)
+        nc.gpsimd.memset(zeros[:], 0.0)
+        nc.scalar.activation(warm[:, 0:1], zeros[:, 0:1], RELU)
 
-        def share_a(i):
-            if i < 8:
-                ix(256 * i + SHARE[i], 256 * i + 256, A)
+        w1_raw = load_rows("w1_raw", w1)
+        x_raw = [load_rows(f"x_raw{a}", xT[:, a:b]) for a, b in X_LOADS[:X_LOADS_BEFORE_W2]]
+        w2_raw = load_rows("w2_raw", w2)
+        x_raw.extend(load_rows(f"x_raw{a}", xT[:, a:b]) for a, b in X_LOADS[X_LOADS_BEFORE_W2:])
+        nc.sync.dma_start(offsets[:], offs)
+        gates = [keep.tile([P, HALF], F32, name=f"gate{i}", align_bytes=64) for i in range(2)]
+        for i in range(2):
+            nc.sync.dma_start(out=gates[i][:], in_=gate[0:P, HALF * i : HALF * (i + 1)])
 
-        for i in range(LA):
-            share_a(i)
-        for i in range(11):
-            j = i - LAG
-            if i < 8:
-                ix(256 * i, 256 * i + SHARE[i], V)
-            if i == 0:
-                qw1()
-            if i == W2S:
-                if W2V > 0:
-                    iw2(0, W2V, V)
-                if W2V < 256:
-                    iw2(W2V, 256, A)
-            if 0 <= j < 8:
-                qh(256 * j, 256 * j + 256)
-            share_a(i + LA)
-            if i < 8:
-                qx(256 * i, 256 * i + 256)
-            if i == W2S:
-                qw2()
-            r = i - LR
-            if 0 <= r < 8:
-                b1(256 * r, (2 * r) % 8)
-                b1(256 * r + 128, (2 * r + 1) % 8)
-            for n, (a, b, at, bk) in enumerate(YAT):
-                if at == i:
-                    b2(a, b, bk)
-        for a, b, blk in SC:
-            sc(a, b, blk)
-            if b == 1024:
-                st(blk, 0, 1024)
-            if b == 2048:
-                st(blk, 1024, 4096)
+        nc.vector.memset(windows[0][:], 0.0)
+        nc.vector.memset(windows[1][:, 0 : T - SCALAR_CLEARS], 0.0)
+        nc.scalar.copy(
+            out=windows[1][:, T - SCALAR_CLEARS : T].rearrange("p (r c) -> p r c", c=ZERO_COLUMNS),
+            in_=zeros[:].unsqueeze(1).to_broadcast([P, SCALAR_CLEARS // ZERO_COLUMNS, ZERO_COLUMNS]),
+        )
+
+        weave_w1(nc.vector.tensor_copy, 0, W1_VECTOR_COLUMNS)
+        weave_w1(nc.scalar.copy, W1_VECTOR_COLUMNS, H)
+        for piece in range(PIECES):
+            a, b = PIECE * piece, PIECE * (piece + 1)
+            split = b - SCALAR_ENTRIES if piece < PIECES - 1 else b
+            if split < b:
+                weave_x(nc.scalar.copy, split, b)
+            weave_x(nc.vector.tensor_copy, a, split)
+            if piece == 0:
+                quantise(w1_codes[:], w1_scales[:], w1_woven[:].rearrange("p t m j -> p (t m j)"))
+            quantise_piece(x_codes, x_scales, x_woven, piece)
+            if piece == W2_AFTER_PIECE:
+                weave(nc.vector.tensor_copy, w2_woven[:], w2_raw[:])
+                quantise(w2_codes[:], w2_scales[:], w2_woven[:].rearrange("p n j -> p (n j)"))
+
+        first_half = [(chunk, block) for block in range(2) for chunk in range(2)]
+        for piece in range(PIECES):
+            layer1(PIECE * piece)
+            layer1(PIECE * piece + P)
+            quantise_piece(h_codes, h_scales, h_woven, piece)
+            if piece >= PIECES // 2:
+                layer2(*first_half[piece - PIECES // 2], 2 * (piece - 1) % BANKS)
+        for n, (chunk, block) in enumerate(first_half):
+            layer2(chunk + 2, block, 2 * n + 1)
+
+        for block in range(2):
+            scatter(block, 0, CHUNK)
+            scatter(block, CHUNK, HALF)
+            store(block, 0, HALF)
+        for block in range(2):
+            scatter(block, HALF, S)
+            store(block, HALF, T)

@@ -24,9 +24,12 @@ HALF = S // 2
 X_LOADS = ((0, 256), (256, 768), (768, 1280), (1280, 1792), (1792, 2048))
 X_LOADS_BEFORE_W2 = 3
 W2_AFTER_PIECE = 4
+GATE_LOADS = ((0, CHUNK), (CHUNK, HALF), (HALF, S))
 SCALAR_CLEARS = 1024
-W1_VECTOR_COLUMNS = 352
+W1_VECTOR_COLUMNS = 320
 SCALAR_ENTRIES = 64
+SCALAR_PIECES = 3
+W2_VECTOR_COLUMNS = 128
 ZERO_COLUMNS = 64
 
 
@@ -104,11 +107,20 @@ def tile_picked_place_mlp_relu_srt_l_kernel(tc, xT, w1, w2, gate, offs, out):
             product(banks[bank][:], w2_codes, w2_scales, block, h_codes, h_scales, a, a + CHUNK)
             nc.scalar.copy(out=y[:, block, a : a + CHUNK], in_=banks[bank][:])
 
+        def load_gate(a, b):
+            tile = keep.tile([P, b - a], F32, name=f"gate{a}", align_bytes=64)
+            nc.sync.dma_start(out=tile[:], in_=gate[0:P, a:b])
+            return tile
+
+        def gate_part(a, b):
+            first, tile = [(lo, t) for (lo, hi), t in zip(GATE_LOADS, gates) if lo <= a and b <= hi][0]
+            return tile[:, a - first : b - first]
+
         def scatter(block, a, b):
             nc.vector.tensor_tensor(
                 windows[block][:].indirect(offsets[:, a // 16 : b // 16]),
                 y[:, block, a:b],
-                gates[a // HALF][:, a % HALF : a % HALF + b - a],
+                gate_part(a, b),
                 MULT,
             )
 
@@ -123,9 +135,7 @@ def tile_picked_place_mlp_relu_srt_l_kernel(tc, xT, w1, w2, gate, offs, out):
         w2_raw = load_rows("w2_raw", w2)
         x_raw.extend(load_rows(f"x_raw{a}", xT[:, a:b]) for a, b in X_LOADS[X_LOADS_BEFORE_W2:])
         nc.sync.dma_start(offsets[:], offs)
-        gates = [keep.tile([P, HALF], F32, name=f"gate{i}", align_bytes=64) for i in range(2)]
-        for i in range(2):
-            nc.sync.dma_start(out=gates[i][:], in_=gate[0:P, HALF * i : HALF * (i + 1)])
+        gates = [load_gate(a, b) for a, b in GATE_LOADS]
 
         nc.vector.memset(windows[0][:], 0.0)
         nc.vector.memset(windows[1][:, 0 : T - SCALAR_CLEARS], 0.0)
@@ -138,7 +148,7 @@ def tile_picked_place_mlp_relu_srt_l_kernel(tc, xT, w1, w2, gate, offs, out):
         weave_w1(nc.scalar.copy, W1_VECTOR_COLUMNS, H)
         for piece in range(PIECES):
             a, b = PIECE * piece, PIECE * (piece + 1)
-            split = b - SCALAR_ENTRIES if piece < PIECES - 1 else b
+            split = b - SCALAR_ENTRIES if piece < SCALAR_PIECES else b
             if split < b:
                 weave_x(nc.scalar.copy, split, b)
             weave_x(nc.vector.tensor_copy, a, split)
@@ -146,7 +156,8 @@ def tile_picked_place_mlp_relu_srt_l_kernel(tc, xT, w1, w2, gate, offs, out):
                 quantise(w1_codes[:], w1_scales[:], w1_woven[:].rearrange("p t m j -> p (t m j)"))
             quantise_piece(x_codes, x_scales, x_woven, piece)
             if piece == W2_AFTER_PIECE:
-                weave(nc.vector.tensor_copy, w2_woven[:], w2_raw[:])
+                weave(nc.vector.tensor_copy, w2_woven[:, 0:W2_VECTOR_COLUMNS, :], w2_raw[:, :, 0:W2_VECTOR_COLUMNS])
+                weave(nc.scalar.copy, w2_woven[:, W2_VECTOR_COLUMNS:N, :], w2_raw[:, :, W2_VECTOR_COLUMNS:N])
                 quantise(w2_codes[:], w2_scales[:], w2_woven[:].rearrange("p n j -> p (n j)"))
 
         first_half = [(chunk, block) for block in range(2) for chunk in range(2)]
@@ -163,6 +174,8 @@ def tile_picked_place_mlp_relu_srt_l_kernel(tc, xT, w1, w2, gate, offs, out):
             scatter(block, 0, CHUNK)
             scatter(block, CHUNK, HALF)
             store(block, 0, HALF)
-        for block in range(2):
-            scatter(block, HALF, S)
-            store(block, HALF, T)
+        scatter(0, HALF, HALF + CHUNK)
+        scatter(0, HALF + CHUNK, S)
+        store(0, HALF, T)
+        scatter(1, HALF, S)
+        store(1, HALF, T)

@@ -21,15 +21,15 @@ PIECE = 256
 CHUNK = 512
 PIECES = S // PIECE
 HALF = S // 2
-X_LOADS = ((0, 256), (256, 768), (768, 1280), (1280, 1792), (1792, 2048))
-X_LOADS_BEFORE_W2 = 3
-W2_AFTER_PIECE = 4
+X_LOADS = tuple((a, a + PIECE) for a in range(0, S, PIECE))
 GATE_LOADS = ((0, CHUNK), (CHUNK, HALF), (HALF, S))
-SCALAR_CLEARS = 1024
-W1_VECTOR_COLUMNS = 320
-SCALAR_ENTRIES = 64
-SCALAR_PIECES = 3
-W2_VECTOR_COLUMNS = 128
+W2_AFTER_PIECE = 3
+AHEAD = 2
+FIRST_Y_PIECE = 3
+SCALAR_CLEARS = 1536
+W1_VECTOR_COLUMNS = 352
+SHARED_PIECES = (0, 1, PIECES - 2, PIECES - 1)
+
 ZERO_COLUMNS = 64
 
 
@@ -131,11 +131,15 @@ def tile_picked_place_mlp_relu_srt_l_kernel(tc, xT, w1, w2, gate, offs, out):
         nc.scalar.activation(warm[:, 0:1], zeros[:, 0:1], RELU)
 
         w1_raw = load_rows("w1_raw", w1)
-        x_raw = [load_rows(f"x_raw{a}", xT[:, a:b]) for a, b in X_LOADS[:X_LOADS_BEFORE_W2]]
-        w2_raw = load_rows("w2_raw", w2)
-        x_raw.extend(load_rows(f"x_raw{a}", xT[:, a:b]) for a, b in X_LOADS[X_LOADS_BEFORE_W2:])
-        nc.sync.dma_start(offsets[:], offs)
-        gates = [load_gate(a, b) for a, b in GATE_LOADS]
+        x_raw, gates = [], []
+        for piece, (a, b) in enumerate(X_LOADS):
+            if piece == PIECES - 1:
+                nc.sync.dma_start(offsets[:], offs)
+                gates.append(load_gate(*GATE_LOADS[0]))
+            x_raw.append(load_rows(f"x_raw{a}", xT[:, a:b]))
+            if piece == W2_AFTER_PIECE:
+                w2_raw = load_rows("w2_raw", w2)
+        gates.extend(load_gate(a, b) for a, b in GATE_LOADS[1:])
 
         nc.vector.memset(windows[0][:], 0.0)
         nc.vector.memset(windows[1][:, 0 : T - SCALAR_CLEARS], 0.0)
@@ -144,31 +148,37 @@ def tile_picked_place_mlp_relu_srt_l_kernel(tc, xT, w1, w2, gate, offs, out):
             in_=zeros[:].unsqueeze(1).to_broadcast([P, SCALAR_CLEARS // ZERO_COLUMNS, ZERO_COLUMNS]),
         )
 
-        weave_w1(nc.vector.tensor_copy, 0, W1_VECTOR_COLUMNS)
-        weave_w1(nc.scalar.copy, W1_VECTOR_COLUMNS, H)
-        for piece in range(PIECES):
+        def weave_piece(piece):
             a, b = PIECE * piece, PIECE * (piece + 1)
-            split = b - SCALAR_ENTRIES if piece < SCALAR_PIECES else b
+            split = a + PIECE // 2 if piece in SHARED_PIECES else b
             if split < b:
                 weave_x(nc.scalar.copy, split, b)
             weave_x(nc.vector.tensor_copy, a, split)
-            if piece == 0:
-                quantise(w1_codes[:], w1_scales[:], w1_woven[:].rearrange("p t m j -> p (t m j)"))
-            quantise_piece(x_codes, x_scales, x_woven, piece)
-            if piece == W2_AFTER_PIECE:
-                weave(nc.vector.tensor_copy, w2_woven[:, 0:W2_VECTOR_COLUMNS, :], w2_raw[:, :, 0:W2_VECTOR_COLUMNS])
-                weave(nc.scalar.copy, w2_woven[:, W2_VECTOR_COLUMNS:N, :], w2_raw[:, :, W2_VECTOR_COLUMNS:N])
-                quantise(w2_codes[:], w2_scales[:], w2_woven[:].rearrange("p n j -> p (n j)"))
+
+        weave_w1(nc.vector.tensor_copy, 0, W1_VECTOR_COLUMNS)
+        weave_w1(nc.scalar.copy, W1_VECTOR_COLUMNS, H)
+        weave_piece(0)
+        quantise(w1_codes[:], w1_scales[:], w1_woven[:].rearrange("p t m j -> p (t m j)"))
+        quantise_piece(x_codes, x_scales, x_woven, 0)
+        weave_piece(1)
+        quantise_piece(x_codes, x_scales, x_woven, 1)
 
         first_half = [(chunk, block) for block in range(2) for chunk in range(2)]
         for piece in range(PIECES):
+            if piece + AHEAD < PIECES:
+                weave_piece(piece + AHEAD)
+                quantise_piece(x_codes, x_scales, x_woven, piece + AHEAD)
+            if piece == 1:
+                weave(nc.vector.tensor_copy, w2_woven[:], w2_raw[:])
+                quantise(w2_codes[:], w2_scales[:], w2_woven[:].rearrange("p n j -> p (n j)"))
             layer1(PIECE * piece)
             layer1(PIECE * piece + P)
             quantise_piece(h_codes, h_scales, h_woven, piece)
-            if piece >= PIECES // 2:
-                layer2(*first_half[piece - PIECES // 2], 2 * (piece - 1) % BANKS)
-        for n, (chunk, block) in enumerate(first_half):
-            layer2(chunk + 2, block, 2 * n + 1)
+            if 0 <= piece - FIRST_Y_PIECE < len(first_half):
+                layer2(*first_half[piece - FIRST_Y_PIECE], 2 * (piece - 1) % BANKS)
+        second_half = [(chunk, block) for chunk in range(2, 4) for block in range(2)]
+        for n, (chunk, block) in enumerate(second_half):
+            layer2(chunk, block, (2 * n + 3) % BANKS)
 
         for block in range(2):
             scatter(block, 0, CHUNK)

@@ -21,14 +21,14 @@ PIECE = 256
 CHUNK = 512
 PIECES = S // PIECE
 HALF = S // 2
-X_LOADS = tuple((a, a + PIECE) for a in range(0, S, PIECE))
+X_LOADS = ((0, 512), (512, 1024), (1024, 1536), (1536, 1792), (1792, 2048))
 GATE_LOADS = ((0, CHUNK), (CHUNK, HALF), (HALF, S))
-W2_AFTER_PIECE = 3
+W2_AFTER_LOAD = 1
 AHEAD = 2
 FIRST_Y_PIECE = 3
-SCALAR_CLEARS = 1536
-W1_VECTOR_COLUMNS = 352
-SHARED_PIECES = (0, 1, PIECES - 2, PIECES - 1)
+SCALAR_CLEARS = 1024
+W1_VECTOR_COLUMNS = 320
+SCALAR_ENTRIES = {1: PIECE, PIECES - 2: PIECE // 2, PIECES - 1: PIECE // 2}
 
 ZERO_COLUMNS = 64
 
@@ -132,12 +132,12 @@ def tile_picked_place_mlp_relu_srt_l_kernel(tc, xT, w1, w2, gate, offs, out):
 
         w1_raw = load_rows("w1_raw", w1)
         x_raw, gates = [], []
-        for piece, (a, b) in enumerate(X_LOADS):
-            if piece == PIECES - 1:
+        for n, (a, b) in enumerate(X_LOADS):
+            if b == S:
                 nc.sync.dma_start(offsets[:], offs)
                 gates.append(load_gate(*GATE_LOADS[0]))
             x_raw.append(load_rows(f"x_raw{a}", xT[:, a:b]))
-            if piece == W2_AFTER_PIECE:
+            if n == W2_AFTER_LOAD:
                 w2_raw = load_rows("w2_raw", w2)
         gates.extend(load_gate(a, b) for a, b in GATE_LOADS[1:])
 
@@ -150,10 +150,11 @@ def tile_picked_place_mlp_relu_srt_l_kernel(tc, xT, w1, w2, gate, offs, out):
 
         def weave_piece(piece):
             a, b = PIECE * piece, PIECE * (piece + 1)
-            split = a + PIECE // 2 if piece in SHARED_PIECES else b
+            split = b - SCALAR_ENTRIES.get(piece, 0)
             if split < b:
                 weave_x(nc.scalar.copy, split, b)
-            weave_x(nc.vector.tensor_copy, a, split)
+            if a < split:
+                weave_x(nc.vector.tensor_copy, a, split)
 
         weave_w1(nc.vector.tensor_copy, 0, W1_VECTOR_COLUMNS)
         weave_w1(nc.scalar.copy, W1_VECTOR_COLUMNS, H)

@@ -21,14 +21,16 @@ PIECE = 256
 CHUNK = 512
 PIECES = S // PIECE
 HALF = S // 2
-X_LOADS = ((0, 512), (512, 1024), (1024, 1536), (1536, 1792), (1792, 2048))
+X_LOADS = ((0, 256), (256, 768), (768, 1280), (1280, 1792), (1792, 2048))
+W2_AFTER_LOAD = 2
 GATE_LOADS = ((0, CHUNK), (CHUNK, HALF), (HALF, S))
-W2_AFTER_LOAD = 1
 AHEAD = 2
 FIRST_Y_PIECE = 3
 SCALAR_CLEARS = 1024
 W1_VECTOR_COLUMNS = 320
-SCALAR_ENTRIES = {1: PIECE, PIECES - 2: PIECE // 2, PIECES - 1: PIECE // 2}
+W2_VECTOR_COLUMNS = 128
+EARLY_PIECES = 3
+LATE_PIECES = 2
 
 ZERO_COLUMNS = 64
 
@@ -58,7 +60,6 @@ def tile_picked_place_mlp_relu_srt_l_kernel(tc, xT, w1, w2, gate, offs, out):
         h_scales = keep.tile([P, S], U8, name="h_scales", align_bytes=64)
         y = keep.tile([P, 2, S], F32, name="y", align_bytes=64)
         zeros = keep.tile([P, ZERO_COLUMNS], F32, name="zeros", align_bytes=64)
-        warm = keep.tile([P, 8], F32, name="warm")
 
         def load_rows(name, src):
             raw = keep.tile([P, PACK, src.shape[1]], F32, name=name, align_bytes=64)
@@ -128,7 +129,6 @@ def tile_picked_place_mlp_relu_srt_l_kernel(tc, xT, w1, w2, gate, offs, out):
             nc.sync.dma_start(out=out_blocks[block, :, a:b], in_=windows[block][:, a:b])
 
         nc.gpsimd.memset(zeros[:], 0.0)
-        nc.scalar.activation(warm[:, 0:1], zeros[:, 0:1], RELU)
 
         w1_raw = load_rows("w1_raw", w1)
         x_raw, gates = [], []
@@ -143,18 +143,19 @@ def tile_picked_place_mlp_relu_srt_l_kernel(tc, xT, w1, w2, gate, offs, out):
 
         nc.vector.memset(windows[0][:], 0.0)
         nc.vector.memset(windows[1][:, 0 : T - SCALAR_CLEARS], 0.0)
-        nc.scalar.copy(
-            out=windows[1][:, T - SCALAR_CLEARS : T].rearrange("p (r c) -> p r c", c=ZERO_COLUMNS),
-            in_=zeros[:].unsqueeze(1).to_broadcast([P, SCALAR_CLEARS // ZERO_COLUMNS, ZERO_COLUMNS]),
+        nc.scalar.activation(
+            windows[1][:, T - SCALAR_CLEARS : T].rearrange("p (r c) -> p r c", c=ZERO_COLUMNS),
+            zeros[:].unsqueeze(1).to_broadcast([P, SCALAR_CLEARS // ZERO_COLUMNS, ZERO_COLUMNS]),
+            RELU,
         )
 
         def weave_piece(piece):
             a, b = PIECE * piece, PIECE * (piece + 1)
-            split = b - SCALAR_ENTRIES.get(piece, 0)
+            early, late = piece < EARLY_PIECES, piece >= PIECES - LATE_PIECES
+            split = b - (PIECE // 4 if early else PIECE // 2 if late else 0)
             if split < b:
                 weave_x(nc.scalar.copy, split, b)
-            if a < split:
-                weave_x(nc.vector.tensor_copy, a, split)
+            weave_x(nc.vector.tensor_copy, a, split)
 
         weave_w1(nc.vector.tensor_copy, 0, W1_VECTOR_COLUMNS)
         weave_w1(nc.scalar.copy, W1_VECTOR_COLUMNS, H)
@@ -170,7 +171,8 @@ def tile_picked_place_mlp_relu_srt_l_kernel(tc, xT, w1, w2, gate, offs, out):
                 weave_piece(piece + AHEAD)
                 quantise_piece(x_codes, x_scales, x_woven, piece + AHEAD)
             if piece == 1:
-                weave(nc.vector.tensor_copy, w2_woven[:], w2_raw[:])
+                weave(nc.vector.tensor_copy, w2_woven[:, 0:W2_VECTOR_COLUMNS, :], w2_raw[:, :, 0:W2_VECTOR_COLUMNS])
+                weave(nc.scalar.copy, w2_woven[:, W2_VECTOR_COLUMNS:N, :], w2_raw[:, :, W2_VECTOR_COLUMNS:N])
                 quantise(w2_codes[:], w2_scales[:], w2_woven[:].rearrange("p n j -> p (n j)"))
             layer1(PIECE * piece)
             layer1(PIECE * piece + P)

@@ -128,6 +128,11 @@ def tile_picked_place_mlp_relu_srt_l_kernel(tc, xT, w1, w2, gate, offs, out):
         def store(block, a, b):
             nc.sync.dma_start(out=out_blocks[block, :, a:b], in_=windows[block][:, a:b])
 
+        def store_on_two_queues(block):
+            middle = (HALF + T) // 2
+            store(block, HALF, middle)
+            nc.scalar.dma_start(out=out_blocks[block, :, middle:T], in_=windows[block][:, middle:T])
+
         nc.gpsimd.memset(zeros[:], 0.0)
 
         w1_raw = load_rows("w1_raw", w1)
@@ -189,6 +194,6 @@ def tile_picked_place_mlp_relu_srt_l_kernel(tc, xT, w1, w2, gate, offs, out):
             store(block, 0, HALF)
         scatter(0, HALF, HALF + CHUNK)
         scatter(0, HALF + CHUNK, S)
-        store(0, HALF, T)
+        store_on_two_queues(0)
         scatter(1, HALF, S)
-        store(1, HALF, T)
+        store_on_two_queues(1)

@@ -33,6 +33,7 @@ EARLY_PIECES = 3
 LATE_PIECES = 2
 
 ZERO_COLUMNS = 64
+DMA_ALIGN = 256
 
 
 def tile_picked_place_mlp_relu_srt_l_kernel(tc, xT, w1, w2, gate, offs, out):
@@ -45,7 +46,7 @@ def tile_picked_place_mlp_relu_srt_l_kernel(tc, xT, w1, w2, gate, offs, out):
         banks = [acc.tile([P, CHUNK], F32, name=f"bank{i}") for i in range(BANKS)]
 
         offsets = keep.tile([P, S // 16], U16, name="offsets")
-        windows = [keep.tile([P, T], F32, name=f"window{b}", align_bytes=64) for b in range(2)]
+        windows = [keep.tile([P, T], F32, name=f"window{b}", align_bytes=DMA_ALIGN) for b in range(2)]
         w1_woven = keep.tile([P, PACK, P, PACK], BF16, name="w1_woven", align_bytes=64)
         w1_codes = keep.tile([P, H], U32, name="w1_codes", align_bytes=64)
         w1_scales = keep.tile([P, H], U8, name="w1_scales", align_bytes=64)
@@ -62,7 +63,7 @@ def tile_picked_place_mlp_relu_srt_l_kernel(tc, xT, w1, w2, gate, offs, out):
         zeros = keep.tile([P, ZERO_COLUMNS], F32, name="zeros", align_bytes=64)
 
         def load_rows(name, src):
-            raw = keep.tile([P, PACK, src.shape[1]], F32, name=name, align_bytes=64)
+            raw = keep.tile([P, PACK, src.shape[1]], F32, name=name, align_bytes=DMA_ALIGN)
             nc.sync.dma_start(out=raw[:], in_=src.rearrange("(p j) c -> p j c", j=PACK))
             return raw
 
@@ -109,7 +110,7 @@ def tile_picked_place_mlp_relu_srt_l_kernel(tc, xT, w1, w2, gate, offs, out):
             nc.scalar.copy(out=y[:, block, a : a + CHUNK], in_=banks[bank][:])
 
         def load_gate(a, b):
-            tile = keep.tile([P, b - a], F32, name=f"gate{a}", align_bytes=64)
+            tile = keep.tile([P, b - a], F32, name=f"gate{a}", align_bytes=DMA_ALIGN)
             nc.sync.dma_start(out=tile[:], in_=gate[0:P, a:b])
             return tile
 

@@ -102,7 +102,11 @@ def tile_picked_place_mlp_relu_srt_l_kernel(tc, xT, w1, w2, gate, offs, out):
             bank = banks[a // P % BANKS][:].rearrange("p (t n) -> p t n", t=PACK)
             for t in range(PACK):
                 product(bank[:, t, :], w1_codes, w1_scales, t, x_codes, x_scales, a, a + P)
-            nc.scalar.activation(h_woven[:, a : a + P, :], bank.rearrange("p t n -> p n t"), RELU)
+            nc.scalar.activation(
+                h_woven[:, a : a + P, :].rearrange("p (n i) t -> p n t i", i=2),
+                bank.rearrange("p t (n i) -> p n t i", i=2),
+                RELU,
+            )
 
         def layer2(chunk, block, bank):
             a = CHUNK * chunk

from contextlib import ExitStack

import concourse.mybir as mybir

K, T, S, H, N = 512, 4096, 2048, 512, 256
FLOPS = 2 * S * (K * H + H * N)

F32 = mybir.dt.float32
BF16 = mybir.dt.bfloat16
U32 = mybir.dt.uint32
U16 = mybir.dt.uint16
U8 = mybir.dt.uint8
FP8X4 = mybir.dt.float8_e4m3fn_x4
RELU = mybir.ActivationFunctionType.Relu
MULT = mybir.AluOpType.mult

P = 128
PACK = 4
BANKS = 8
PIECE = 256
CHUNK = 512
PIECES = S // PIECE
HALF = S // 2
X_LOADS = ((0, 256), (256, 768), (768, 1280), (1280, 1792), (1792, 2048))
W2_AFTER_LOAD = 2
GATE_LOADS = ((0, CHUNK), (CHUNK, HALF), (HALF, S))
AHEAD = 2
FIRST_Y_PIECE = 3
SCALAR_CLEARS = 1024
W1_VECTOR_COLUMNS = 320
W2_VECTOR_COLUMNS = 128
EARLY_PIECES = 3
LATE_PIECES = 2

ZERO_COLUMNS = 64
DMA_ALIGN = 256


def tile_picked_place_mlp_relu_srt_l_kernel(tc, xT, w1, w2, gate, offs, out):
    nc = tc.nc
    out_blocks = out.rearrange("(b p) t -> b p t", p=P)

    with ExitStack() as ctx:
        keep = ctx.enter_context(tc.tile_pool(name="keep", bufs=1))
        acc = ctx.enter_context(tc.psum_pool(name="acc", bufs=1))
        banks = [acc.tile([P, CHUNK], F32, name=f"bank{i}") for i in range(BANKS)]

        offsets = keep.tile([P, S // 16], U16, name="offsets")
        windows = [keep.tile([P, T], F32, name=f"window{b}", align_bytes=DMA_ALIGN) for b in range(2)]
        w1_woven = keep.tile([P, PACK, P, PACK], BF16, name="w1_woven", align_bytes=64)
        w1_codes = keep.tile([P, H], U32, name="w1_codes", align_bytes=64)
        w1_scales = keep.tile([P, H], U8, name="w1_scales", align_bytes=64)
        w2_woven = keep.tile([P, N, PACK], BF16, name="w2_woven", align_bytes=64)
        w2_codes = keep.tile([P, N], U32, name="w2_codes", align_bytes=64)
        w2_scales = keep.tile([P, N], U8, name="w2_scales", align_bytes=64)
        x_woven = keep.tile([P, S, PACK], BF16, name="x_woven", align_bytes=64)
        x_codes = keep.tile([P, S], U32, name="x_codes", align_bytes=64)
        x_scales = keep.tile([P, S], U8, name="x_scales", align_bytes=64)
        h_woven = keep.tile([P, S, PACK], BF16, name="h_woven", align_bytes=64)
        h_codes = keep.tile([P, S], U32, name="h_codes", align_bytes=64)
        h_scales = keep.tile([P, S], U8, name="h_scales", align_bytes=64)
        y = keep.tile([P, 2, S], F32, name="y", align_bytes=64)
        zeros = keep.tile([P, ZERO_COLUMNS], F32, name="zeros", align_bytes=64)

        def load_rows(name, src):
            raw = keep.tile([P, PACK, src.shape[1]], F32, name=name, align_bytes=DMA_ALIGN)
            nc.sync.dma_start(out=raw[:], in_=src.rearrange("(p j) c -> p j c", j=PACK))
            return raw

        def weave(copy, dst, src):
            copy(out=dst.rearrange("p (c i) j -> p c j i", i=2), in_=src.rearrange("p j (c i) -> p c j i", i=2))

        def weave_w1(copy, a, b):
            copy(
                out=w1_woven[:, :, a // PACK : b // PACK, :].rearrange("p t m j -> p m t j"),
                in_=w1_raw[:, :, a:b].rearrange("p j (m t) -> p m t j", t=PACK),
            )

        def weave_x(copy, a, b):
            first, raw = [(lo, t) for (lo, hi), t in zip(X_LOADS, x_raw) if lo <= a and b <= hi][0]
            weave(copy, x_woven[:, a:b, :], raw[:, :, a - first : b - first])

        def quantise(codes, scales, woven):
            nc.vector.quantize_mx(out=codes.bitcast(FP8X4), scales=scales, in_=woven)

        def quantise_piece(codes, scales, woven, piece):
            cols = slice(PIECE * piece, PIECE * (piece + 1))
            quantise(codes[:, cols], scales[:, cols], woven[:, cols, :].rearrange("p n j -> p (n j)"))

        def product(dst, w_codes, w_scales, group, codes, scales, a, b):
            nc.tensor.matmul_mx(
                out=dst,
                lhsT=w_codes[:, P * group : P * (group + 1)].bitcast(FP8X4),
                lhsT_scale=w_scales[:, P * group : P * (group + 1)],
                rhs=codes[:, a:b].bitcast(FP8X4),
                rhs_scale=scales[:, a:b],
                start=True,
                stop=True,
            )

        def layer1(a):
            bank = banks[a // P % BANKS][:].rearrange("p (t n) -> p t n", t=PACK)
            for t in range(PACK):
                product(bank[:, t, :], w1_codes, w1_scales, t, x_codes, x_scales, a, a + P)
            nc.scalar.activation(
                h_woven[:, a : a + P, :].rearrange("p (n i) t -> p n t i", i=2),
                bank.rearrange("p t (n i) -> p n t i", i=2),
                RELU,
            )

        def layer2(chunk, block, bank):
            a = CHUNK * chunk
            product(banks[bank][:], w2_codes, w2_scales, block, h_codes, h_scales, a, a + CHUNK)
            nc.scalar.copy(out=y[:, block, a : a + CHUNK], in_=banks[bank][:])

        def load_gate(a, b):
            tile = keep.tile([P, b - a], F32, name=f"gate{a}", align_bytes=DMA_ALIGN)
            nc.sync.dma_start(out=tile[:], in_=gate[0:P, a:b])
            return tile

        def gate_part(a, b):
            first, tile = [(lo, t) for (lo, hi), t in zip(GATE_LOADS, gates) if lo <= a and b <= hi][0]
            return tile[:, a - first : b - first]

        def scatter(block, a, b):
            nc.vector.tensor_tensor(
                windows[block][:].indirect(offsets[:, a // 16 : b // 16]),
                y[:, block, a:b],
                gate_part(a, b),
                MULT,
            )

        def store(block, a, b):
            nc.sync.dma_start(out=out_blocks[block, :, a:b], in_=windows[block][:, a:b])

        def store_on_two_queues(block):
            middle = (HALF + T) // 2
            store(block, HALF, middle)
            nc.scalar.dma_start(out=out_blocks[block, :, middle:T], in_=windows[block][:, middle:T])

        nc.gpsimd.memset(zeros[:], 0.0)

        w1_raw = load_rows("w1_raw", w1)
        x_raw, gates = [], []
        for n, (a, b) in enumerate(X_LOADS):
            if b == S:
                nc.sync.dma_start(offsets[:], offs)
                gates.append(load_gate(*GATE_LOADS[0]))
            x_raw.append(load_rows(f"x_raw{a}", xT[:, a:b]))
            if n == W2_AFTER_LOAD:
                w2_raw = load_rows("w2_raw", w2)
        gates.extend(load_gate(a, b) for a, b in GATE_LOADS[1:])

        nc.vector.memset(windows[0][:], 0.0)
        nc.vector.memset(windows[1][:, 0 : T - SCALAR_CLEARS], 0.0)
        nc.scalar.activation(
            windows[1][:, T - SCALAR_CLEARS : T].rearrange("p (r c) -> p r c", c=ZERO_COLUMNS),
            zeros[:].unsqueeze(1).to_broadcast([P, SCALAR_CLEARS // ZERO_COLUMNS, ZERO_COLUMNS]),
            RELU,
        )

        def weave_piece(piece):
            a, b = PIECE * piece, PIECE * (piece + 1)
            early, late = piece < EARLY_PIECES, piece >= PIECES - LATE_PIECES
            split = b - (PIECE // 4 if early else PIECE // 2 if late else 0)
            if split < b:
                weave_x(nc.scalar.copy, split, b)
            weave_x(nc.vector.tensor_copy, a, split)

        weave_w1(nc.vector.tensor_copy, 0, W1_VECTOR_COLUMNS)
        weave_w1(nc.scalar.copy, W1_VECTOR_COLUMNS, H)
        weave_piece(0)
        quantise(w1_codes[:], w1_scales[:], w1_woven[:].rearrange("p t m j -> p (t m j)"))
        quantise_piece(x_codes, x_scales, x_woven, 0)
        weave_piece(1)
        quantise_piece(x_codes, x_scales, x_woven, 1)

        first_half = [(chunk, block) for block in range(2) for chunk in range(2)]
        for piece in range(PIECES):
            if piece + AHEAD < PIECES:
                weave_piece(piece + AHEAD)
                quantise_piece(x_codes, x_scales, x_woven, piece + AHEAD)
            if piece == 1:
                weave(nc.vector.tensor_copy, w2_woven[:, 0:W2_VECTOR_COLUMNS, :], w2_raw[:, :, 0:W2_VECTOR_COLUMNS])
                weave(nc.scalar.copy, w2_woven[:, W2_VECTOR_COLUMNS:N, :], w2_raw[:, :, W2_VECTOR_COLUMNS:N])
                quantise(w2_codes[:], w2_scales[:], w2_woven[:].rearrange("p n j -> p (n j)"))
            layer1(PIECE * piece)
            layer1(PIECE * piece + P)
            quantise_piece(h_codes, h_scales, h_woven, piece)
            if 0 <= piece - FIRST_Y_PIECE < len(first_half):
                layer2(*first_half[piece - FIRST_Y_PIECE], 2 * (piece - 1) % BANKS)
        second_half = [(chunk, block) for chunk in range(2, 4) for block in range(2)]
        for n, (chunk, block) in enumerate(second_half):
            layer2(chunk, block, (2 * n + 3) % BANKS)

        for block in range(2):
            scatter(block, 0, CHUNK)
            scatter(block, CHUNK, HALF)
            store(block, 0, HALF)
        scatter(0, HALF, HALF + CHUNK)
        scatter(0, HALF + CHUNK, S)
        store_on_two_queues(0)
        scatter(1, HALF, S)
        store_on_two_queues(1)
